import numpy as np
import ml_dtypes


def mxq(x, axis, fmt="e4m3"):
    dtype, down = {"e4m3": (ml_dtypes.float8_e4m3fn, 7), "e5m2": (ml_dtypes.float8_e5m2, 14)}[fmt]
    v = np.moveaxis(np.asarray(x, np.float32).astype(ml_dtypes.bfloat16).astype(np.float64), axis, -1)
    blocks = v.reshape(v.shape[:-1] + (-1, 32))
    amax = np.abs(blocks).max(-1, keepdims=True)
    byte = np.maximum(np.where(amax > 0, np.frexp(amax)[1] - 1 + 127, 0) - down, 1)
    scale = np.exp2(byte - 127.0)
    codes = (blocks / scale).astype(np.float32).astype(dtype).astype(np.float64)
    return np.moveaxis((codes * scale).reshape(v.shape), -1, axis)


WIDE = False


def mx_kscale(k):
    if not WIDE:
        return np.ones(k)
    levels = np.array([10, -10, 5, -5, 0])
    if k % 512:
        return np.exp2(np.random.permutation(np.resize(levels, k // 32))).repeat(32)
    a = np.empty((k // 512, 16))
    for p in range(k // 512):
        a[p, :8] = np.random.permutation(np.resize(levels, 8))
        for g in range(8):
            far = levels[np.abs(levels - a[p, g]) >= 10]
            a[p, g + 8] = far[np.random.randint(len(far))]
    return np.exp2(a.ravel()).repeat(32)


def f64(x):
    return np.asarray(x).astype(np.float64)


def striped(idx):
    return np.tile(idx.reshape(-1, 16).T, (8, 1)).astype(np.uint16)


def unstriped(offs):
    return offs[:16].T.reshape(-1).astype(np.int64)


def pack_weight(w):
    k, n = w.shape
    w = f64(np.asarray(w, np.float32).astype(ml_dtypes.bfloat16)).reshape(k // 32, 32, n)
    amax = np.abs(w).max(1)
    byte = np.clip(np.where(amax > 0, np.frexp(amax)[1] - 1 + 127 - 7, 1), 1, 254)
    scaled = (w * np.exp2(127.0 - byte)[:, None, :]).reshape(k, n).astype(np.float32)
    words = np.ascontiguousarray(scaled.reshape(k // 512, 128, 4, n).transpose(0, 1, 3, 2)).astype(ml_dtypes.float8_e4m3fn).view(np.uint8)
    return words, np.ascontiguousarray(byte.astype(np.uint8).reshape(k // 512, 16, n))


def unpack_weight(words, scales):
    g, p, n, _ = words.shape
    vals = np.ascontiguousarray(words).view(ml_dtypes.float8_e4m3fn).astype(np.float64) * np.repeat(np.exp2(scales.astype(np.float64) - 127.0), 8, axis=1)[..., None]
    return vals.transpose(0, 1, 3, 2).reshape(g * 512, n)


def planes(y):
    n, m = y.shape
    v = y.astype(np.float32).astype(ml_dtypes.bfloat16).astype(np.float64).reshape(n // 32, 32, m)
    top = np.abs(v).max(1)
    byte = np.clip(np.where(top > 0, np.frexp(top)[1] - 1 + 127 - 7, 1), 1, 254)
    codes = (v * np.exp2(127.0 - byte)[:, None, :]).reshape(n, m).astype(np.float32).astype(ml_dtypes.float8_e4m3fn).view(np.uint8)
    words = codes.reshape(n // 512, 128, 4, m).transpose(0, 1, 3, 2)
    return np.ascontiguousarray(words), np.ascontiguousarray(byte.astype(np.uint8).reshape(n // 512, 16, m))


def gelu(v):
    return 0.5 * v * (1.0 + np.tanh(np.sqrt(2.0 / np.pi) * (v + 0.044715 * v**3)))


K, T, S, J = 512, 2048, 512, 512


def setup_inputs():
    n = np.random.standard_normal
    s = mx_kscale(K)[:, None]
    packed_xT = pack_weight(n((K, T)) * s)
    return {
        "x_words": packed_xT[0],
        "x_scales": packed_xT[1],
        "hT": (n((K, J)) / np.sqrt(K) / s).astype(np.float32),
        "bias": (0.5 * n((S, 1))).astype(np.float32),
        "offs": striped(np.random.permutation(T)[:S]),
    }


def reference(x_words, x_scales, hT, bias, offs):
    xq = unpack_weight(x_words, x_scales)[:, unstriped(offs)]
    hTq = mxq(f64(hT), 0, "e4m3")
    out_0 = gelu((xq.T @ hTq) + f64(bias))
    return (out_0,) + planes(out_0)

@@ -1,0 +1,120 @@
+from contextlib import ExitStack
+
+import concourse.mybir as mybir
+
+K, T, S, J = 512, 2048, 512, 512
+FLOPS = 2 * K * S * J
+
+F32 = mybir.dt.float32
+BF16 = mybir.dt.bfloat16
+I32 = mybir.dt.int32
+U32 = mybir.dt.uint32
+U16 = mybir.dt.uint16
+U8 = mybir.dt.uint8
+FP8X4 = mybir.dt.float8_e4m3fn_x4
+GELU = mybir.ActivationFunctionType.Gelu_apprx_tanh
+
+P = 128
+PACK = 4
+QUADS = 4
+WIDTHS = (128, 128, 128, 128)
+ON_SCALAR = 3
+
+
+def interleave(copy, dst, src):
+    copy(
+        out=dst[:].rearrange("p (c i t) -> p c t i", i=4, t=PACK),
+        in_=src[:].rearrange("p t (c i) -> p c t i", i=4),
+    )
+
+
+def tile_picked_zdeja_bias_po_kernel(tc, x_words, x_scales, hT, bias, offs, out_0, out_1, out_2):
+    nc = tc.nc
+    with ExitStack() as ctx:
+        keep = ctx.enter_context(tc.tile_pool(name="keep", bufs=1))
+        psum = ctx.enter_context(tc.psum_pool(name="psum", bufs=1))
+
+        starts = [sum(WIDTHS[:c]) for c in range(len(WIDTHS))]
+        h_rows = hT.rearrange("(p t) j -> p t j", t=PACK)
+        h_raw = [keep.tile([P, PACK, w], F32, name=f"h_raw{c}") for c, w in enumerate(WIDTHS)]
+
+        def load_h(c):
+            nc.sync.dma_start(out=h_raw[c][:], in_=h_rows[:, :, starts[c] : starts[c] + WIDTHS[c]])
+
+        table_scales = keep.tile([P, T], U8, name="table_scales", align_bytes=64)
+        nc.vector.memset(table_scales[:].bitcast(I32), 0)
+        load_h(0)
+        offsets = keep.tile([P, S // 16], U16, name="offsets")
+        nc.sync.dma_start(offsets[:], offs)
+        for r in range(4):
+            nc.sync.dma_start(
+                out=table_scales[r:P:32, :].bitcast(I32),
+                in_=x_scales[0, r:16:4, :].bitcast(I32),
+            )
+        table_words = keep.tile([P, T], U32, name="table_words", align_bytes=64)
+        nc.sync.dma_start(
+            out=table_words[:].bitcast(I32),
+            in_=x_words[0].rearrange("p c r -> p (c r)").bitcast(I32),
+        )
+        for c in range(1, len(WIDTHS)):
+            load_h(c)
+        bias_sb = keep.tile([P, PACK], F32, name="bias_sb")
+        nc.scalar.dma_start(out=bias_sb[:], in_=bias.rearrange("(p t) o -> p (t o)", t=PACK))
+
+        picked_scales = keep.tile([P, S], U8, name="picked_scales", align_bytes=64)
+        nc.vector.tensor_copy(out=picked_scales[:], in_=table_scales[:].indirect(offsets[:]))
+        x_scale = keep.tile([P, S], U8, name="x_scale", align_bytes=64)
+        nc.vector.tensor_copy(
+            out=x_scale[:].rearrange("p (t m) -> p t m", t=PACK),
+            in_=picked_scales[:].rearrange("p (m t) -> p t m", t=PACK),
+        )
+        x_codes = keep.tile([P, S], U32, name="x_codes", align_bytes=64)
+        nc.vector.tensor_copy(
+            out=x_codes[:].rearrange("p (t m) -> p m t", t=PACK),
+            in_=table_words[:].indirect(offsets[:]),
+        )
+
+        y_codes = keep.tile([P, J], U32, name="y_codes", align_bytes=64)
+        y_scale = keep.tile([P, J], U8, name="y_scale", align_bytes=64)
+        y_rows = out_0.rearrange("(p t) j -> p t j", t=PACK)
+        words_out = out_1[0].rearrange("p c r -> p (c r)").bitcast(I32)
+
+        h_q = []
+        for c, w in enumerate(WIDTHS):
+            h_bf = keep.tile([P, PACK * w], BF16, name=f"h_bf{c}", align_bytes=64)
+            interleave(nc.scalar.copy if c < ON_SCALAR else nc.vector.tensor_copy, h_bf, h_raw[c])
+            h_codes = keep.tile([P, w], U32, name=f"h_codes{c}", align_bytes=64)
+            h_scale = keep.tile([P, w], U8, name=f"h_scale{c}", align_bytes=64)
+            nc.vector.quantize_mx(out=h_codes[:].bitcast(FP8X4), scales=h_scale[:], in_=h_bf[:])
+            h_q.append((h_codes, h_scale))
+
+        for c, w in enumerate(WIDTHS):
+            cols = slice(starts[c], starts[c] + w)
+            h_codes, h_scale = h_q[c]
+            y = keep.tile([P, PACK, w], F32, name=f"y{c}")
+            for t in range(PACK):
+                acc = psum.tile([P, w], F32, name=f"acc{c % 2}_{t}")
+                m_cols = slice(t * P, (t + 1) * P)
+                nc.tensor.matmul_mx(
+                    out=acc[:],
+                    lhsT=x_codes[:, m_cols].bitcast(FP8X4),
+                    lhsT_scale=x_scale[:, m_cols],
+                    rhs=h_codes[:].bitcast(FP8X4),
+                    rhs_scale=h_scale[:],
+                    start=True,
+                    stop=True,
+                )
+                nc.scalar.activation(out=y[:, t, :], in_=acc[:], func=GELU, bias=bias_sb[:, t : t + 1])
+            nc.sync.dma_start(out=y_rows[:, :, cols], in_=y[:])
+            y_bf = keep.tile([P, PACK * w], BF16, name=f"y_bf{c}", align_bytes=64)
+            interleave(nc.vector.tensor_copy, y_bf, y)
+            nc.vector.quantize_mx(out=y_codes[:, cols].bitcast(FP8X4), scales=y_scale[:, cols], in_=y_bf[:])
+            if c % 2 == 1:
+                pair = slice(starts[c - 1], starts[c] + w)
+                nc.sync.dma_start(out=words_out[:, pair], in_=y_codes[:, pair].bitcast(I32))
+        for q in range(QUADS):
+            queue = nc.scalar if q % 2 == 0 else nc.sync
+            queue.dma_start(
+                out=out_2[0, 4 * q : 4 * q + 4, :].bitcast(I32),
+                in_=y_scale[32 * q : 32 * q + 4, :].bitcast(I32),
+            )

@@ -18,7 +18,7 @@ P = 128
 PACK = 4
 QUADS = 4
 WIDTHS = (128, 128, 128, 128)
-ON_SCALAR = 3
+ON_SCALAR = 2
 
 
 def interleave(copy, dst, src):
@@ -46,8 +46,11 @@ def tile_picked_zdeja_bias_po_kernel(tc, x_words, x_scales, hT, bias, offs, out_
         load_h(0)
         offsets = keep.tile([P, S // 16], U16, name="offsets")
         nc.sync.dma_start(offsets[:], offs)
+        bias_sb = keep.tile([P, PACK], F32, name="bias_sb")
+        nc.scalar.dma_start(out=bias_sb[:], in_=bias.rearrange("(p t) o -> p (t o)", t=PACK))
         for r in range(4):
-            nc.sync.dma_start(
+            queue = nc.scalar if r % 2 == 0 else nc.sync
+            queue.dma_start(
                 out=table_scales[r:P:32, :].bitcast(I32),
                 in_=x_scales[0, r:16:4, :].bitcast(I32),
             )
@@ -58,8 +61,8 @@ def tile_picked_zdeja_bias_po_kernel(tc, x_words, x_scales, hT, bias, offs, out_
         )
         for c in range(1, len(WIDTHS)):
             load_h(c)
-        bias_sb = keep.tile([P, PACK], F32, name="bias_sb")
-        nc.scalar.dma_start(out=bias_sb[:], in_=bias.rearrange("(p t) o -> p (t o)", t=PACK))
+        warm = keep.tile([P, PACK], F32, name="warm")
+        nc.scalar.activation(out=warm[:], in_=bias_sb[:], func=GELU)
 
         picked_scales = keep.tile([P, S], U8, name="picked_scales", align_bytes=64)
         nc.vector.tensor_copy(out=picked_scales[:], in_=table_scales[:].indirect(offsets[:]))

@@ -16,15 +16,15 @@ GELU = mybir.ActivationFunctionType.Gelu_apprx_tanh
 
 P = 128
 PACK = 4
-QUADS = 4
-WIDTHS = (128, 128, 128, 128)
-ON_SCALAR = 2
+W = 128
+CHUNKS = J // W
+LAST = CHUNKS - 1
 
 
 def interleave(copy, dst, src):
     copy(
-        out=dst[:].rearrange("p (c i t) -> p c t i", i=4, t=PACK),
-        in_=src[:].rearrange("p t (c i) -> p c t i", i=4),
+        out=dst.rearrange("p (c i t) -> p c t i", i=4, t=PACK),
+        in_=src.rearrange("p t (c i) -> p c t i", i=4),
     )
 
 
@@ -34,23 +34,14 @@ def tile_picked_zdeja_bias_po_kernel(tc, x_words, x_scales, hT, bias, offs, out_
         keep = ctx.enter_context(tc.tile_pool(name="keep", bufs=1))
         psum = ctx.enter_context(tc.psum_pool(name="psum", bufs=1))
 
-        starts = [sum(WIDTHS[:c]) for c in range(len(WIDTHS))]
-        h_rows = hT.rearrange("(p t) j -> p t j", t=PACK)
-        h_raw = [keep.tile([P, PACK, w], F32, name=f"h_raw{c}") for c, w in enumerate(WIDTHS)]
-
-        def load_h(c):
-            nc.sync.dma_start(out=h_raw[c][:], in_=h_rows[:, :, starts[c] : starts[c] + WIDTHS[c]])
-
-        table_scales = keep.tile([P, T], U8, name="table_scales", align_bytes=64)
-        nc.vector.memset(table_scales[:].bitcast(I32), 0)
-        load_h(0)
         offsets = keep.tile([P, S // 16], U16, name="offsets")
         nc.sync.dma_start(offsets[:], offs)
+        table_scales = keep.tile([P, T], U8, name="table_scales", align_bytes=64)
+        nc.vector.memset(table_scales[:].bitcast(I32), 0)
         bias_sb = keep.tile([P, PACK], F32, name="bias_sb")
-        nc.scalar.dma_start(out=bias_sb[:], in_=bias.rearrange("(p t) o -> p (t o)", t=PACK))
+        nc.sync.dma_start(out=bias_sb[:], in_=bias.rearrange("(p t) o -> p (t o)", t=PACK))
         for r in range(4):
-            queue = nc.scalar if r % 2 == 0 else nc.sync
-            queue.dma_start(
+            nc.sync.dma_start(
                 out=table_scales[r:P:32, :].bitcast(I32),
                 in_=x_scales[0, r:16:4, :].bitcast(I32),
             )
@@ -59,8 +50,13 @@ def tile_picked_zdeja_bias_po_kernel(tc, x_words, x_scales, hT, bias, offs, out_
             out=table_words[:].bitcast(I32),
             in_=x_words[0].rearrange("p c r -> p (c r)").bitcast(I32),
         )
-        for c in range(1, len(WIDTHS)):
-            load_h(c)
+        h_rows = hT.rearrange("(p t) j -> p t j", t=PACK)
+        h_raw = []
+        for c in range(CHUNKS):
+            raw = keep.tile([P, PACK, W], F32, name=f"h_raw{c}", tag=f"f32_{c}")
+            nc.sync.dma_start(out=raw[:], in_=h_rows[:, :, c * W : (c + 1) * W])
+            h_raw.append(raw)
+
         warm = keep.tile([P, PACK], F32, name="warm")
         nc.scalar.activation(out=warm[:], in_=bias_sb[:], func=GELU)
 
@@ -71,51 +67,69 @@ def tile_picked_zdeja_bias_po_kernel(tc, x_words, x_scales, hT, bias, offs, out_
             out=x_scale[:].rearrange("p (t m) -> p t m", t=PACK),
             in_=picked_scales[:].rearrange("p (m t) -> p t m", t=PACK),
         )
-        x_codes = keep.tile([P, S], U32, name="x_codes", align_bytes=64)
+        picked_words = keep.tile([P, S], U32, name="picked_words", align_bytes=64)
+        nc.vector.tensor_copy(out=picked_words[:], in_=table_words[:].indirect(offsets[:]))
+
+        h_bf, h_codes, h_scale = {}, {}, {}
+
+        def round_h(c):
+            h_bf[c] = keep.tile([P, PACK * W], BF16, name=f"h_bf{c}", tag=f"bf_{c}", align_bytes=64)
+            interleave(nc.vector.tensor_copy if c == LAST else nc.scalar.copy, h_bf[c][:], h_raw[c][:])
+
+        def quantize_h(c):
+            h_codes[c] = keep.tile([P, W], U32, name=f"h_codes{c}", align_bytes=64)
+            h_scale[c] = keep.tile([P, W], U8, name=f"h_scale{c}", align_bytes=64)
+            nc.vector.quantize_mx(out=h_codes[c][:].bitcast(FP8X4), scales=h_scale[c][:], in_=h_bf[c][:])
+
+        for c in range(LAST):
+            round_h(c)
+        quantize_h(0)
+        x_codes = keep.tile([P, S], U32, name="x_codes", tag="bf_0", align_bytes=64)
         nc.vector.tensor_copy(
-            out=x_codes[:].rearrange("p (t m) -> p m t", t=PACK),
-            in_=table_words[:].indirect(offsets[:]),
+            out=x_codes[:].rearrange("p (t c i) -> p c t i", t=PACK, i=4),
+            in_=picked_words[:].rearrange("p (c i t) -> p c t i", t=PACK, i=4),
         )
+        quantize_h(1)
+        round_h(LAST)
+        for c in range(2, CHUNKS):
+            quantize_h(c)
 
         y_codes = keep.tile([P, J], U32, name="y_codes", align_bytes=64)
         y_scale = keep.tile([P, J], U8, name="y_scale", align_bytes=64)
+        y_bf = keep.tile([P, PACK * J], BF16, name="y_bf", tag=f"bf_{LAST}", align_bytes=64)
         y_rows = out_0.rearrange("(p t) j -> p t j", t=PACK)
         words_out = out_1[0].rearrange("p c r -> p (c r)").bitcast(I32)
 
-        h_q = []
-        for c, w in enumerate(WIDTHS):
-            h_bf = keep.tile([P, PACK * w], BF16, name=f"h_bf{c}", align_bytes=64)
-            interleave(nc.scalar.copy if c < ON_SCALAR else nc.vector.tensor_copy, h_bf, h_raw[c])
-            h_codes = keep.tile([P, w], U32, name=f"h_codes{c}", align_bytes=64)
-            h_scale = keep.tile([P, w], U8, name=f"h_scale{c}", align_bytes=64)
-            nc.vector.quantize_mx(out=h_codes[:].bitcast(FP8X4), scales=h_scale[:], in_=h_bf[:])
-            h_q.append((h_codes, h_scale))
-
-        for c, w in enumerate(WIDTHS):
-            cols = slice(starts[c], starts[c] + w)
-            h_codes, h_scale = h_q[c]
-            y = keep.tile([P, PACK, w], F32, name=f"y{c}")
+        for c in range(CHUNKS):
+            cols = slice(c * W, (c + 1) * W)
+            y = keep.tile([P, PACK, W], F32, name=f"y{c}", tag=f"f32_{(c + 2) % CHUNKS}")
             for t in range(PACK):
-                acc = psum.tile([P, w], F32, name=f"acc{c % 2}_{t}")
+                acc = psum.tile([P, W], F32, name=f"acc{c % 2}_{t}")
                 m_cols = slice(t * P, (t + 1) * P)
                 nc.tensor.matmul_mx(
                     out=acc[:],
                     lhsT=x_codes[:, m_cols].bitcast(FP8X4),
                     lhsT_scale=x_scale[:, m_cols],
-                    rhs=h_codes[:].bitcast(FP8X4),
-                    rhs_scale=h_scale[:],
+                    rhs=h_codes[c][:].bitcast(FP8X4),
+                    rhs_scale=h_scale[c][:],
                     start=True,
                     stop=True,
                 )
                 nc.scalar.activation(out=y[:, t, :], in_=acc[:], func=GELU, bias=bias_sb[:, t : t + 1])
             nc.sync.dma_start(out=y_rows[:, :, cols], in_=y[:])
-            y_bf = keep.tile([P, PACK * w], BF16, name=f"y_bf{c}", align_bytes=64)
-            interleave(nc.vector.tensor_copy, y_bf, y)
-            nc.vector.quantize_mx(out=y_codes[:, cols].bitcast(FP8X4), scales=y_scale[:, cols], in_=y_bf[:])
+            interleave(nc.vector.tensor_copy, y_bf[:, PACK * c * W : PACK * (c + 1) * W], y[:])
+            if c >= 1:
+                first = 0 if c == 1 else c * W
+                span = slice(first, (c + 1) * W)
+                nc.vector.quantize_mx(
+                    out=y_codes[:, span].bitcast(FP8X4),
+                    scales=y_scale[:, span],
+                    in_=y_bf[:, PACK * first : PACK * (c + 1) * W],
+                )
             if c % 2 == 1:
-                pair = slice(starts[c - 1], starts[c] + w)
+                pair = slice((c - 1) * W, (c + 1) * W)
                 nc.sync.dma_start(out=words_out[:, pair], in_=y_codes[:, pair].bitcast(I32))
-        for q in range(QUADS):
+        for q in range(4):
             queue = nc.scalar if q % 2 == 0 else nc.sync
             queue.dma_start(
                 out=out_2[0, 4 * q : 4 * q + 4, :].bitcast(I32),

@@ -19,6 +19,8 @@ PACK = 4
 W = 128
 CHUNKS = J // W
 LAST = CHUNKS - 1
+HEAD = 256
+ON_SCALAR = 2
 
 
 def interleave(copy, dst, src):
@@ -34,6 +36,9 @@ def tile_picked_zdeja_bias_po_kernel(tc, x_words, x_scales, hT, bias, offs, out_
         keep = ctx.enter_context(tc.tile_pool(name="keep", bufs=1))
         psum = ctx.enter_context(tc.psum_pool(name="psum", bufs=1))
 
+        table_words = keep.tile([P, T], U32, name="table_words", align_bytes=64)
+        words_in = x_words[0].rearrange("p c r -> p (c r)").bitcast(I32)
+        nc.sync.dma_start(out=table_words[:, :HEAD].bitcast(I32), in_=words_in[:, :HEAD])
         offsets = keep.tile([P, S // 16], U16, name="offsets")
         nc.sync.dma_start(offsets[:], offs)
         table_scales = keep.tile([P, T], U8, name="table_scales", align_bytes=64)
@@ -45,15 +50,11 @@ def tile_picked_zdeja_bias_po_kernel(tc, x_words, x_scales, hT, bias, offs, out_
                 out=table_scales[r:P:32, :].bitcast(I32),
                 in_=x_scales[0, r:16:4, :].bitcast(I32),
             )
-        table_words = keep.tile([P, T], U32, name="table_words", align_bytes=64)
-        nc.sync.dma_start(
-            out=table_words[:].bitcast(I32),
-            in_=x_words[0].rearrange("p c r -> p (c r)").bitcast(I32),
-        )
+        nc.sync.dma_start(out=table_words[:, HEAD:].bitcast(I32), in_=words_in[:, HEAD:])
         h_rows = hT.rearrange("(p t) j -> p t j", t=PACK)
         h_raw = []
         for c in range(CHUNKS):
-            raw = keep.tile([P, PACK, W], F32, name=f"h_raw{c}", tag=f"f32_{c}")
+            raw = keep.tile([P, PACK, W], F32, name=f"h_raw{c}", tag=f"f32_{c}", align_bytes=64)
             nc.sync.dma_start(out=raw[:], in_=h_rows[:, :, c * W : (c + 1) * W])
             h_raw.append(raw)
 
@@ -74,14 +75,14 @@ def tile_picked_zdeja_bias_po_kernel(tc, x_words, x_scales, hT, bias, offs, out_
 
         def round_h(c):
             h_bf[c] = keep.tile([P, PACK * W], BF16, name=f"h_bf{c}", tag=f"bf_{c}", align_bytes=64)
-            interleave(nc.vector.tensor_copy if c == LAST else nc.scalar.copy, h_bf[c][:], h_raw[c][:])
+            interleave(nc.scalar.copy if c < ON_SCALAR else nc.vector.tensor_copy, h_bf[c][:], h_raw[c][:])
 
         def quantize_h(c):
             h_codes[c] = keep.tile([P, W], U32, name=f"h_codes{c}", align_bytes=64)
             h_scale[c] = keep.tile([P, W], U8, name=f"h_scale{c}", align_bytes=64)
             nc.vector.quantize_mx(out=h_codes[c][:].bitcast(FP8X4), scales=h_scale[c][:], in_=h_bf[c][:])
 
-        for c in range(LAST):
+        for c in range(ON_SCALAR):
             round_h(c)
         quantize_h(0)
         x_codes = keep.tile([P, S], U32, name="x_codes", tag="bf_0", align_bytes=64)
@@ -90,19 +91,19 @@ def tile_picked_zdeja_bias_po_kernel(tc, x_words, x_scales, hT, bias, offs, out_
             in_=picked_words[:].rearrange("p (c i t) -> p c t i", t=PACK, i=4),
         )
         quantize_h(1)
-        round_h(LAST)
-        for c in range(2, CHUNKS):
+        for c in range(ON_SCALAR, CHUNKS):
+            round_h(c)
             quantize_h(c)
 
         y_codes = keep.tile([P, J], U32, name="y_codes", align_bytes=64)
         y_scale = keep.tile([P, J], U8, name="y_scale", align_bytes=64)
-        y_bf = keep.tile([P, PACK * J], BF16, name="y_bf", tag=f"bf_{LAST}", align_bytes=64)
+        y_bf = keep.tile([P, PACK * J], BF16, name="y_bf", tag=f"f32_{LAST}", align_bytes=64)
         y_rows = out_0.rearrange("(p t) j -> p t j", t=PACK)
         words_out = out_1[0].rearrange("p c r -> p (c r)").bitcast(I32)
 
         for c in range(CHUNKS):
             cols = slice(c * W, (c + 1) * W)
-            y = keep.tile([P, PACK, W], F32, name=f"y{c}", tag=f"f32_{(c + 2) % CHUNKS}")
+            y = keep.tile([P, PACK, W], F32, name=f"y{c}", tag=f"f32_{ON_SCALAR - 1}" if c == 0 else f"y{c}", align_bytes=64)
             for t in range(PACK):
                 acc = psum.tile([P, W], F32, name=f"acc{c % 2}_{t}")
                 m_cols = slice(t * P, (t + 1) * P)
@@ -116,7 +117,10 @@ def tile_picked_zdeja_bias_po_kernel(tc, x_words, x_scales, hT, bias, offs, out_
                     stop=True,
                 )
                 nc.scalar.activation(out=y[:, t, :], in_=acc[:], func=GELU, bias=bias_sb[:, t : t + 1])
-            nc.sync.dma_start(out=y_rows[:, :, cols], in_=y[:])
+                rows = 2 if c < 2 else PACK
+                if (t + 1) % rows == 0:
+                    done = slice(t + 1 - rows, t + 1)
+                    nc.sync.dma_start(out=y_rows[:, done, cols], in_=y[:, done, :])
             interleave(nc.vector.tensor_copy, y_bf[:, PACK * c * W : PACK * (c + 1) * W], y[:])
             if c >= 1:
                 first = 0 if c == 1 else c * W

@@ -21,6 +21,7 @@ CHUNKS = J // W
 LAST = CHUNKS - 1
 HEAD = 256
 ON_SCALAR = 2
+HALVES = 2
 
 
 def interleave(copy, dst, src):
@@ -44,9 +45,9 @@ def tile_picked_zdeja_bias_po_kernel(tc, x_words, x_scales, hT, bias, offs, out_
         table_scales = keep.tile([P, T], U8, name="table_scales", align_bytes=64)
         nc.vector.memset(table_scales[:].bitcast(I32), 0)
         bias_sb = keep.tile([P, PACK], F32, name="bias_sb")
-        nc.sync.dma_start(out=bias_sb[:], in_=bias.rearrange("(p t) o -> p (t o)", t=PACK))
+        nc.scalar.dma_start(out=bias_sb[:], in_=bias.rearrange("(p t) o -> p (t o)", t=PACK))
         for r in range(4):
-            nc.sync.dma_start(
+            (nc.sync if r % 2 == 0 else nc.scalar).dma_start(
                 out=table_scales[r:P:32, :].bitcast(I32),
                 in_=x_scales[0, r:16:4, :].bitcast(I32),
             )
@@ -54,7 +55,7 @@ def tile_picked_zdeja_bias_po_kernel(tc, x_words, x_scales, hT, bias, offs, out_
         h_rows = hT.rearrange("(p t) j -> p t j", t=PACK)
         h_raw = []
         for c in range(CHUNKS):
-            raw = keep.tile([P, PACK, W], F32, name=f"h_raw{c}", tag=f"f32_{c}", align_bytes=64)
+            raw = keep.tile([P, PACK, W], F32, name=f"h_raw{c}", align_bytes=64)
             nc.sync.dma_start(out=raw[:], in_=h_rows[:, :, c * W : (c + 1) * W])
             h_raw.append(raw)
 
@@ -68,67 +69,64 @@ def tile_picked_zdeja_bias_po_kernel(tc, x_words, x_scales, hT, bias, offs, out_
             out=x_scale[:].rearrange("p (t m) -> p t m", t=PACK),
             in_=picked_scales[:].rearrange("p (m t) -> p t m", t=PACK),
         )
-        picked_words = keep.tile([P, S], U32, name="picked_words", align_bytes=64)
-        nc.vector.tensor_copy(out=picked_words[:], in_=table_words[:].indirect(offsets[:]))
+        part = S // HALVES
+        picked_words = []
+        for a in range(HALVES):
+            picked = keep.tile([P, part], U32, name=f"picked_words{a}", align_bytes=64)
+            nc.vector.tensor_copy(out=picked[:], in_=table_words[:].indirect(offsets[:, a * part // 16 : (a + 1) * part // 16]))
+            picked_words.append(picked)
+        x_codes = keep.tile([P, PACK, P], U32, name="x_codes", align_bytes=64)
+        for a in range(HALVES):
+            nc.vector.tensor_copy(
+                out=x_codes[:, :, a * part // PACK : (a + 1) * part // PACK].rearrange("p t (c i) -> p c t i", i=4),
+                in_=picked_words[a][:].rearrange("p (c i t) -> p c t i", t=PACK, i=4),
+            )
 
         h_bf, h_codes, h_scale = {}, {}, {}
-
-        def round_h(c):
+        for c in range(CHUNKS):
             h_bf[c] = keep.tile([P, PACK * W], BF16, name=f"h_bf{c}", tag=f"bf_{c}", align_bytes=64)
             interleave(nc.scalar.copy if c < ON_SCALAR else nc.vector.tensor_copy, h_bf[c][:], h_raw[c][:])
-
-        def quantize_h(c):
+        for c in range(CHUNKS):
             h_codes[c] = keep.tile([P, W], U32, name=f"h_codes{c}", align_bytes=64)
             h_scale[c] = keep.tile([P, W], U8, name=f"h_scale{c}", align_bytes=64)
             nc.vector.quantize_mx(out=h_codes[c][:].bitcast(FP8X4), scales=h_scale[c][:], in_=h_bf[c][:])
 
-        for c in range(ON_SCALAR):
-            round_h(c)
-        quantize_h(0)
-        x_codes = keep.tile([P, S], U32, name="x_codes", tag="bf_0", align_bytes=64)
-        nc.vector.tensor_copy(
-            out=x_codes[:].rearrange("p (t c i) -> p c t i", t=PACK, i=4),
-            in_=picked_words[:].rearrange("p (c i t) -> p c t i", t=PACK, i=4),
-        )
-        quantize_h(1)
-        for c in range(ON_SCALAR, CHUNKS):
-            round_h(c)
-            quantize_h(c)
-
         y_codes = keep.tile([P, J], U32, name="y_codes", align_bytes=64)
         y_scale = keep.tile([P, J], U8, name="y_scale", align_bytes=64)
-        y_bf = keep.tile([P, PACK * J], BF16, name="y_bf", tag=f"f32_{LAST}", align_bytes=64)
+        y_bf = keep.tile([P, PACK * J], BF16, name="y_bf", tag=f"bf_{LAST}", align_bytes=64)
         y_rows = out_0.rearrange("(p t) j -> p t j", t=PACK)
         words_out = out_1[0].rearrange("p c r -> p (c r)").bitcast(I32)
 
         for c in range(CHUNKS):
             cols = slice(c * W, (c + 1) * W)
-            y = keep.tile([P, PACK, W], F32, name=f"y{c}", tag=f"f32_{ON_SCALAR - 1}" if c == 0 else f"y{c}", align_bytes=64)
+            y = keep.tile([P, PACK, W], F32, name=f"y{c}", align_bytes=64)
             for t in range(PACK):
                 acc = psum.tile([P, W], F32, name=f"acc{c % 2}_{t}")
-                m_cols = slice(t * P, (t + 1) * P)
                 nc.tensor.matmul_mx(
                     out=acc[:],
-                    lhsT=x_codes[:, m_cols].bitcast(FP8X4),
-                    lhsT_scale=x_scale[:, m_cols],
+                    lhsT=x_codes[:, t, :].bitcast(FP8X4),
+                    lhsT_scale=x_scale[:, t * P : (t + 1) * P],
                     rhs=h_codes[c][:].bitcast(FP8X4),
                     rhs_scale=h_scale[c][:],
                     start=True,
                     stop=True,
                 )
                 nc.scalar.activation(out=y[:, t, :], in_=acc[:], func=GELU, bias=bias_sb[:, t : t + 1])
-                rows = 2 if c < 2 else PACK
+                rows = 2 if c < 1 else PACK
                 if (t + 1) % rows == 0:
                     done = slice(t + 1 - rows, t + 1)
                     nc.sync.dma_start(out=y_rows[:, done, cols], in_=y[:, done, :])
-            interleave(nc.vector.tensor_copy, y_bf[:, PACK * c * W : PACK * (c + 1) * W], y[:])
-            if c >= 1:
-                first = 0 if c == 1 else c * W
-                span = slice(first, (c + 1) * W)
+            parts = 2 if c == LAST else 1
+            width = W // parts
+            for b in range(parts):
+                first = c * W + b * width
+                interleave(nc.vector.tensor_copy, y_bf[:, PACK * first : PACK * (first + width)], y[:, :, b * width : (b + 1) * width])
+            for b in range(parts):
+                first = c * W + b * width
                 nc.vector.quantize_mx(
-                    out=y_codes[:, span].bitcast(FP8X4),
-                    scales=y_scale[:, span],
-                    in_=y_bf[:, PACK * first : PACK * (c + 1) * W],
+                    out=y_codes[:, first : first + width].bitcast(FP8X4),
+                    scales=y_scale[:, first : first + width],
+                    in_=y_bf[:, PACK * first : PACK * (first + width)],
                 )
             if c % 2 == 1:
                 pair = slice((c - 1) * W, (c + 1) * W)

@@ -45,9 +45,9 @@ def tile_picked_zdeja_bias_po_kernel(tc, x_words, x_scales, hT, bias, offs, out_
         table_scales = keep.tile([P, T], U8, name="table_scales", align_bytes=64)
         nc.vector.memset(table_scales[:].bitcast(I32), 0)
         bias_sb = keep.tile([P, PACK], F32, name="bias_sb")
-        nc.scalar.dma_start(out=bias_sb[:], in_=bias.rearrange("(p t) o -> p (t o)", t=PACK))
+        nc.sync.dma_start(out=bias_sb[:], in_=bias.rearrange("(p t) o -> p (t o)", t=PACK))
         for r in range(4):
-            (nc.sync if r % 2 == 0 else nc.scalar).dma_start(
+            nc.sync.dma_start(
                 out=table_scales[r:P:32, :].bitcast(I32),
                 in_=x_scales[0, r:16:4, :].bitcast(I32),
             )

@@ -19,9 +19,13 @@ PACK = 4
 W = 128
 CHUNKS = J // W
 LAST = CHUNKS - 1
-HEAD = 256
+HEAD = 512
 ON_SCALAR = 2
 HALVES = 2
+GROUPS = ((0, 128), (128, 256), (256, 384), (384, 512))
+STORE_ROWS = (2, 4, 4, 4)
+PARTS = (1, 1, 1, 2)
+WORDS_AFTER = (1, 3)
 
 
 def interleave(copy, dst, src):
@@ -62,14 +66,18 @@ def tile_picked_zdeja_bias_po_kernel(tc, x_words, x_scales, hT, bias, offs, out_
         warm = keep.tile([P, PACK], F32, name="warm")
         nc.scalar.activation(out=warm[:], in_=bias_sb[:], func=GELU)
 
-        picked_scales = keep.tile([P, S], U8, name="picked_scales", align_bytes=64)
-        nc.vector.tensor_copy(out=picked_scales[:], in_=table_scales[:].indirect(offsets[:]))
-        x_scale = keep.tile([P, S], U8, name="x_scale", align_bytes=64)
-        nc.vector.tensor_copy(
-            out=x_scale[:].rearrange("p (t m) -> p t m", t=PACK),
-            in_=picked_scales[:].rearrange("p (m t) -> p t m", t=PACK),
-        )
         part = S // HALVES
+        picked_scales = []
+        for a in range(HALVES):
+            picked = keep.tile([P, part], U8, name=f"picked_scales{a}", align_bytes=64)
+            nc.vector.tensor_copy(out=picked[:], in_=table_scales[:].indirect(offsets[:, a * part // 16 : (a + 1) * part // 16]))
+            picked_scales.append(picked)
+        x_scale = keep.tile([P, S], U8, name="x_scale", align_bytes=64)
+        for a in range(HALVES):
+            nc.vector.tensor_copy(
+                out=x_scale[:].rearrange("p (t m) -> p t m", t=PACK)[:, :, a * part // PACK : (a + 1) * part // PACK],
+                in_=picked_scales[a][:].rearrange("p (m t) -> p t m", t=PACK),
+            )
         picked_words = []
         for a in range(HALVES):
             picked = keep.tile([P, part], U32, name=f"picked_words{a}", align_bytes=64)
@@ -82,14 +90,16 @@ def tile_picked_zdeja_bias_po_kernel(tc, x_words, x_scales, hT, bias, offs, out_
                 in_=picked_words[a][:].rearrange("p (c i t) -> p c t i", t=PACK, i=4),
             )
 
-        h_bf, h_codes, h_scale = {}, {}, {}
+        h_bf = []
         for c in range(CHUNKS):
-            h_bf[c] = keep.tile([P, PACK * W], BF16, name=f"h_bf{c}", tag=f"bf_{c}", align_bytes=64)
-            interleave(nc.scalar.copy if c < ON_SCALAR else nc.vector.tensor_copy, h_bf[c][:], h_raw[c][:])
+            rounded = keep.tile([P, PACK * W], BF16, name=f"h_bf{c}", tag=f"bf_{c}", align_bytes=64)
+            interleave(nc.scalar.copy if c < ON_SCALAR else nc.vector.tensor_copy, rounded[:], h_raw[c][:])
+            h_bf.append(rounded)
+        h_codes = keep.tile([P, J], U32, name="h_codes", align_bytes=64)
+        h_scale = keep.tile([P, J], U8, name="h_scale", align_bytes=64)
         for c in range(CHUNKS):
-            h_codes[c] = keep.tile([P, W], U32, name=f"h_codes{c}", align_bytes=64)
-            h_scale[c] = keep.tile([P, W], U8, name=f"h_scale{c}", align_bytes=64)
-            nc.vector.quantize_mx(out=h_codes[c][:].bitcast(FP8X4), scales=h_scale[c][:], in_=h_bf[c][:])
+            cols = slice(c * W, (c + 1) * W)
+            nc.vector.quantize_mx(out=h_codes[:, cols].bitcast(FP8X4), scales=h_scale[:, cols], in_=h_bf[c][:])
 
         y_codes = keep.tile([P, J], U32, name="y_codes", align_bytes=64)
         y_scale = keep.tile([P, J], U8, name="y_scale", align_bytes=64)
@@ -97,40 +107,39 @@ def tile_picked_zdeja_bias_po_kernel(tc, x_words, x_scales, hT, bias, offs, out_
         y_rows = out_0.rearrange("(p t) j -> p t j", t=PACK)
         words_out = out_1[0].rearrange("p c r -> p (c r)").bitcast(I32)
 
-        for c in range(CHUNKS):
-            cols = slice(c * W, (c + 1) * W)
-            y = keep.tile([P, PACK, W], F32, name=f"y{c}", align_bytes=64)
+        stored = 0
+        for g, (lo, hi) in enumerate(GROUPS):
+            cols = slice(lo, hi)
+            y = keep.tile([P, PACK, hi - lo], F32, name=f"y{g}", align_bytes=64)
             for t in range(PACK):
-                acc = psum.tile([P, W], F32, name=f"acc{c % 2}_{t}")
+                acc = psum.tile([P, hi - lo], F32, name=f"acc{g % 2}_{t}")
                 nc.tensor.matmul_mx(
                     out=acc[:],
                     lhsT=x_codes[:, t, :].bitcast(FP8X4),
                     lhsT_scale=x_scale[:, t * P : (t + 1) * P],
-                    rhs=h_codes[c][:].bitcast(FP8X4),
-                    rhs_scale=h_scale[c][:],
+                    rhs=h_codes[:, cols].bitcast(FP8X4),
+                    rhs_scale=h_scale[:, cols],
                     start=True,
                     stop=True,
                 )
                 nc.scalar.activation(out=y[:, t, :], in_=acc[:], func=GELU, bias=bias_sb[:, t : t + 1])
-                rows = 2 if c < 1 else PACK
-                if (t + 1) % rows == 0:
-                    done = slice(t + 1 - rows, t + 1)
+                if (t + 1) % STORE_ROWS[g] == 0:
+                    done = slice(t + 1 - STORE_ROWS[g], t + 1)
                     nc.sync.dma_start(out=y_rows[:, done, cols], in_=y[:, done, :])
-            parts = 2 if c == LAST else 1
-            width = W // parts
-            for b in range(parts):
-                first = c * W + b * width
+            width = (hi - lo) // PARTS[g]
+            for b in range(PARTS[g]):
+                first = lo + b * width
                 interleave(nc.vector.tensor_copy, y_bf[:, PACK * first : PACK * (first + width)], y[:, :, b * width : (b + 1) * width])
-            for b in range(parts):
-                first = c * W + b * width
+            for b in range(PARTS[g]):
+                first = lo + b * width
                 nc.vector.quantize_mx(
                     out=y_codes[:, first : first + width].bitcast(FP8X4),
                     scales=y_scale[:, first : first + width],
                     in_=y_bf[:, PACK * first : PACK * (first + width)],
                 )
-            if c % 2 == 1:
-                pair = slice((c - 1) * W, (c + 1) * W)
-                nc.sync.dma_start(out=words_out[:, pair], in_=y_codes[:, pair].bitcast(I32))
+            if g in WORDS_AFTER:
+                nc.sync.dma_start(out=words_out[:, stored:hi], in_=y_codes[:, stored:hi].bitcast(I32))
+                stored = hi
         for q in range(4):
             queue = nc.scalar if q % 2 == 0 else nc.sync
             queue.dma_start(

@@ -22,16 +22,23 @@ LAST = CHUNKS - 1
 HEAD = 512
 ON_SCALAR = 2
 HALVES = 2
-GROUPS = ((0, 128), (128, 256), (256, 384), (384, 512))
-STORE_ROWS = (2, 4, 4, 4)
-PARTS = (1, 1, 1, 2)
-WORDS_AFTER = (1, 3)
+FIRST_PARTS = 1
+STORE_ROWS = (2,4,4,4)
+PARTS = (1,1,1,2)
+WORDS_AFTER = (1,3,)
 
 
 def interleave(copy, dst, src):
     copy(
         out=dst.rearrange("p (c i t) -> p c t i", i=4, t=PACK),
         in_=src.rearrange("p t (c i) -> p c t i", i=4),
+    )
+
+
+def interleave_pair(copy, dst, src, u):
+    copy(
+        out=dst.rearrange("p (c i t) -> p c t i", i=4, t=PACK)[:, :, 2 * u : 2 * u + 2, :],
+        in_=src[:, 2 * u : 2 * u + 2, :].rearrange("p t (c i) -> p c t i", i=4),
     )
 
 
@@ -57,10 +64,11 @@ def tile_picked_zdeja_bias_po_kernel(tc, x_words, x_scales, hT, bias, offs, out_
             )
         nc.sync.dma_start(out=table_words[:, HEAD:].bitcast(I32), in_=words_in[:, HEAD:])
         h_rows = hT.rearrange("(p t) j -> p t j", t=PACK)
+        pieces = [(0, b * W // FIRST_PARTS, W // FIRST_PARTS) for b in range(FIRST_PARTS)] + [(c, 0, W) for c in range(1, CHUNKS)]
         h_raw = []
-        for c in range(CHUNKS):
-            raw = keep.tile([P, PACK, W], F32, name=f"h_raw{c}", align_bytes=64)
-            nc.sync.dma_start(out=raw[:], in_=h_rows[:, :, c * W : (c + 1) * W])
+        for c, lo, width in pieces:
+            raw = keep.tile([P, PACK, width], F32, name=f"h_raw{c}_{lo}", tag=f"h_raw{c}_{lo}", align_bytes=64)
+            nc.sync.dma_start(out=raw[:], in_=h_rows[:, :, c * W + lo : c * W + lo + width])
             h_raw.append(raw)
 
         warm = keep.tile([P, PACK], F32, name="warm")
@@ -78,28 +86,38 @@ def tile_picked_zdeja_bias_po_kernel(tc, x_words, x_scales, hT, bias, offs, out_
                 out=x_scale[:].rearrange("p (t m) -> p t m", t=PACK)[:, :, a * part // PACK : (a + 1) * part // PACK],
                 in_=picked_scales[a][:].rearrange("p (m t) -> p t m", t=PACK),
             )
-        picked_words = []
-        for a in range(HALVES):
-            picked = keep.tile([P, part], U32, name=f"picked_words{a}", align_bytes=64)
-            nc.vector.tensor_copy(out=picked[:], in_=table_words[:].indirect(offsets[:, a * part // 16 : (a + 1) * part // 16]))
-            picked_words.append(picked)
-        x_codes = keep.tile([P, PACK, P], U32, name="x_codes", align_bytes=64)
-        for a in range(HALVES):
-            nc.vector.tensor_copy(
-                out=x_codes[:, :, a * part // PACK : (a + 1) * part // PACK].rearrange("p t (c i) -> p c t i", i=4),
-                in_=picked_words[a][:].rearrange("p (c i t) -> p c t i", t=PACK, i=4),
-            )
-
-        h_bf = []
-        for c in range(CHUNKS):
-            rounded = keep.tile([P, PACK * W], BF16, name=f"h_bf{c}", tag=f"bf_{c}", align_bytes=64)
-            interleave(nc.scalar.copy if c < ON_SCALAR else nc.vector.tensor_copy, rounded[:], h_raw[c][:])
-            h_bf.append(rounded)
+        h_bf = [keep.tile([P, PACK * W], BF16, name=f"h_bf{c}", tag=f"bf_{c}", align_bytes=64) for c in range(CHUNKS)]
         h_codes = keep.tile([P, J], U32, name="h_codes", align_bytes=64)
         h_scale = keep.tile([P, J], U8, name="h_scale", align_bytes=64)
-        for c in range(CHUNKS):
+
+        def round_h(n):
+            c, lo, width = pieces[n]
+            interleave(nc.scalar.copy if c < ON_SCALAR else nc.vector.tensor_copy, h_bf[c][:, PACK * lo : PACK * (lo + width)], h_raw[n][:])
+
+        def quantise_h(c):
             cols = slice(c * W, (c + 1) * W)
             nc.vector.quantize_mx(out=h_codes[:, cols].bitcast(FP8X4), scales=h_scale[:, cols], in_=h_bf[c][:])
+
+        picked_words = keep.tile([P, S], U32, name="picked_words", align_bytes=64)
+        nc.vector.tensor_copy(out=picked_words[:], in_=table_words[:].indirect(offsets[:]))
+        x_codes = []
+
+        def deal(u, tag):
+            dealt = keep.tile([P, 2 * P], U32, name=f"x_codes{u}", tag=tag, align_bytes=64)
+            nc.vector.tensor_copy(
+                out=dealt[:].rearrange("p (t c i) -> p c t i", t=2, i=4),
+                in_=picked_words[:].rearrange("p (c i t) -> p c t i", t=PACK, i=4)[:, :, 2 * u : 2 * u + 2, :],
+            )
+            x_codes.extend([dealt[:, :P], dealt[:, P:]])
+
+        deal(0, "x_codes0")
+        round_h(0)
+        quantise_h(0)
+        deal(1, "h_raw0_0")
+        for n in range(1, len(pieces)):
+            round_h(n)
+        for c in range(1, CHUNKS):
+            quantise_h(c)
 
         y_codes = keep.tile([P, J], U32, name="y_codes", align_bytes=64)
         y_scale = keep.tile([P, J], U8, name="y_scale", align_bytes=64)
@@ -108,14 +126,15 @@ def tile_picked_zdeja_bias_po_kernel(tc, x_words, x_scales, hT, bias, offs, out_
         words_out = out_1[0].rearrange("p c r -> p (c r)").bitcast(I32)
 
         stored = 0
-        for g, (lo, hi) in enumerate(GROUPS):
+        for g in range(CHUNKS):
+            lo, hi = g * W, (g + 1) * W
             cols = slice(lo, hi)
-            y = keep.tile([P, PACK, hi - lo], F32, name=f"y{g}", align_bytes=64)
+            y = keep.tile([P, PACK, W], F32, name=f"y{g}", align_bytes=64)
             for t in range(PACK):
-                acc = psum.tile([P, hi - lo], F32, name=f"acc{g % 2}_{t}")
+                acc = psum.tile([P, W], F32, name=f"acc{g % 2}_{t}")
                 nc.tensor.matmul_mx(
                     out=acc[:],
-                    lhsT=x_codes[:, t, :].bitcast(FP8X4),
+                    lhsT=x_codes[t].bitcast(FP8X4),
                     lhsT_scale=x_scale[:, t * P : (t + 1) * P],
                     rhs=h_codes[:, cols].bitcast(FP8X4),
                     rhs_scale=h_scale[:, cols],
@@ -126,10 +145,16 @@ def tile_picked_zdeja_bias_po_kernel(tc, x_words, x_scales, hT, bias, offs, out_
                 if (t + 1) % STORE_ROWS[g] == 0:
                     done = slice(t + 1 - STORE_ROWS[g], t + 1)
                     nc.sync.dma_start(out=y_rows[:, done, cols], in_=y[:, done, :])
-            width = (hi - lo) // PARTS[g]
-            for b in range(PARTS[g]):
-                first = lo + b * width
-                interleave(nc.vector.tensor_copy, y_bf[:, PACK * first : PACK * (first + width)], y[:, :, b * width : (b + 1) * width])
+            width = W // PARTS[g]
+            if g == LAST:
+                for u in range(2):
+                    for b in range(PARTS[g]):
+                        first = lo + b * width
+                        interleave_pair(nc.vector.tensor_copy, y_bf[:, PACK * first : PACK * (first + width)], y[:, :, b * width : (b + 1) * width], u)
+            else:
+                for b in range(PARTS[g]):
+                    first = lo + b * width
+                    interleave(nc.vector.tensor_copy, y_bf[:, PACK * first : PACK * (first + width)], y[:, :, b * width : (b + 1) * width])
             for b in range(PARTS[g]):
                 first = lo + b * width
                 nc.vector.quantize_mx(

@@ -19,7 +19,7 @@ PACK = 4
 W = 128
 CHUNKS = J // W
 LAST = CHUNKS - 1
-HEAD = 512
+HEAD = 768
 ON_SCALAR = 2
 HALVES = 2
 FIRST_PARTS = 1
@@ -56,7 +56,7 @@ def tile_picked_zdeja_bias_po_kernel(tc, x_words, x_scales, hT, bias, offs, out_
         table_scales = keep.tile([P, T], U8, name="table_scales", align_bytes=64)
         nc.vector.memset(table_scales[:].bitcast(I32), 0)
         bias_sb = keep.tile([P, PACK], F32, name="bias_sb")
-        nc.sync.dma_start(out=bias_sb[:], in_=bias.rearrange("(p t) o -> p (t o)", t=PACK))
+        nc.gpsimd.dma_start(out=bias_sb[:], in_=bias.rearrange("(p t) o -> p (t o)", t=PACK))
         for r in range(4):
             nc.sync.dma_start(
                 out=table_scales[r:P:32, :].bitcast(I32),
@@ -71,8 +71,10 @@ def tile_picked_zdeja_bias_po_kernel(tc, x_words, x_scales, hT, bias, offs, out_
             nc.sync.dma_start(out=raw[:], in_=h_rows[:, :, c * W + lo : c * W + lo + width])
             h_raw.append(raw)
 
-        warm = keep.tile([P, PACK], F32, name="warm")
-        nc.scalar.activation(out=warm[:], in_=bias_sb[:], func=GELU)
+        zero = keep.tile([P, 1], F32, name="zero")
+        nc.vector.memset(zero[:], 0.0)
+        warm = keep.tile([P, 1], F32, name="warm")
+        nc.scalar.activation(out=warm[:], in_=zero[:], func=GELU)
 
         part = S // HALVES
         picked_scales = []

@@ -19,26 +19,20 @@ PACK = 4
 W = 128
 CHUNKS = J // W
 LAST = CHUNKS - 1
-HEAD = 768
+HEAD = 128
+ROW0 = 48
 ON_SCALAR = 2
 HALVES = 2
-FIRST_PARTS = 1
 STORE_ROWS = (2,4,4,4)
 PARTS = (1,1,1,2)
 WORDS_AFTER = (1,3,)
 
 
-def interleave(copy, dst, src):
+def interleave(copy, dst, src, t0=0):
+    rows = src.shape[1]
     copy(
-        out=dst.rearrange("p (c i t) -> p c t i", i=4, t=PACK),
+        out=dst.rearrange("p (c i t) -> p c t i", i=4, t=PACK)[:, :, t0 : t0 + rows, :],
         in_=src.rearrange("p t (c i) -> p c t i", i=4),
-    )
-
-
-def interleave_pair(copy, dst, src, u):
-    copy(
-        out=dst.rearrange("p (c i t) -> p c t i", i=4, t=PACK)[:, :, 2 * u : 2 * u + 2, :],
-        in_=src[:, 2 * u : 2 * u + 2, :].rearrange("p t (c i) -> p c t i", i=4),
     )
 
 
@@ -51,26 +45,29 @@ def tile_picked_zdeja_bias_po_kernel(tc, x_words, x_scales, hT, bias, offs, out_
         table_words = keep.tile([P, T], U32, name="table_words", align_bytes=64)
         words_in = x_words[0].rearrange("p c r -> p (c r)").bitcast(I32)
         nc.sync.dma_start(out=table_words[:, :HEAD].bitcast(I32), in_=words_in[:, :HEAD])
+        table_scales = keep.tile([P, T], U8, name="table_scales", align_bytes=64)
+        nc.sync.dma_start(out=table_scales[ROW0 : ROW0 + 16, :].bitcast(I32), in_=x_scales[0].bitcast(I32))
         offsets = keep.tile([P, S // 16], U16, name="offsets")
         nc.sync.dma_start(offsets[:], offs)
-        table_scales = keep.tile([P, T], U8, name="table_scales", align_bytes=64)
-        nc.vector.memset(table_scales[:].bitcast(I32), 0)
+        nc.vector.memset(table_scales[:ROW0, :].bitcast(I32), 0)
+        nc.vector.memset(table_scales[ROW0 + 16 :, :].bitcast(I32), 0)
         bias_sb = keep.tile([P, PACK], F32, name="bias_sb")
         nc.gpsimd.dma_start(out=bias_sb[:], in_=bias.rearrange("(p t) o -> p (t o)", t=PACK))
-        for r in range(4):
-            nc.sync.dma_start(
-                out=table_scales[r:P:32, :].bitcast(I32),
-                in_=x_scales[0, r:16:4, :].bitcast(I32),
-            )
         nc.sync.dma_start(out=table_words[:, HEAD:].bitcast(I32), in_=words_in[:, HEAD:])
         h_rows = hT.rearrange("(p t) j -> p t j", t=PACK)
-        pieces = [(0, b * W // FIRST_PARTS, W // FIRST_PARTS) for b in range(FIRST_PARTS)] + [(c, 0, W) for c in range(1, CHUNKS)]
+        pieces = [(c, 0, PACK) for c in range(CHUNKS)]
         h_raw = []
-        for c, lo, width in pieces:
-            raw = keep.tile([P, PACK, width], F32, name=f"h_raw{c}_{lo}", tag=f"h_raw{c}_{lo}", align_bytes=64)
-            nc.sync.dma_start(out=raw[:], in_=h_rows[:, :, c * W + lo : c * W + lo + width])
+
+        def load_h(c, tag):
+            raw = keep.tile([P, PACK, W], F32, name=f"h_raw{c}", tag=tag, align_bytes=64)
+            nc.sync.dma_start(out=raw[:], in_=h_rows[:, :, c * W : (c + 1) * W])
             h_raw.append(raw)
 
+        for c in range(3):
+            load_h(c, f"raw{c}")
+
+        x_scale = keep.tile([P, S], U8, name="x_scale", align_bytes=64)
+        nc.vector.memset(x_scale[:].bitcast(I32), 0)
         zero = keep.tile([P, 1], F32, name="zero")
         nc.vector.memset(zero[:], 0.0)
         warm = keep.tile([P, 1], F32, name="warm")
@@ -79,22 +76,29 @@ def tile_picked_zdeja_bias_po_kernel(tc, x_words, x_scales, hT, bias, offs, out_
         part = S // HALVES
         picked_scales = []
         for a in range(HALVES):
-            picked = keep.tile([P, part], U8, name=f"picked_scales{a}", align_bytes=64)
+            picked = keep.tile([P, part], U8, name=f"picked_scales{a}", tag=f"picked{a}", align_bytes=64)
             nc.vector.tensor_copy(out=picked[:], in_=table_scales[:].indirect(offsets[:, a * part // 16 : (a + 1) * part // 16]))
             picked_scales.append(picked)
-        x_scale = keep.tile([P, S], U8, name="x_scale", align_bytes=64)
+        dealt_scales = keep.tile([P, S], U8, name="dealt_scales", align_bytes=64)
         for a in range(HALVES):
             nc.vector.tensor_copy(
-                out=x_scale[:].rearrange("p (t m) -> p t m", t=PACK)[:, :, a * part // PACK : (a + 1) * part // PACK],
+                out=dealt_scales[:].rearrange("p (t m) -> p t m", t=PACK)[:, :, a * part // PACK : (a + 1) * part // PACK],
                 in_=picked_scales[a][:].rearrange("p (m t) -> p t m", t=PACK),
             )
+        for r in range(4):
+            nc.sync.dma_start(
+                out=x_scale[r:P:32, :].bitcast(I32),
+                in_=dealt_scales[ROW0 + r : ROW0 + 16 : 4, :].bitcast(I32),
+            )
+        for c in range(3, CHUNKS):
+            load_h(c, f"picked{CHUNKS - c}" if c < LAST else "picked1")
         h_bf = [keep.tile([P, PACK * W], BF16, name=f"h_bf{c}", tag=f"bf_{c}", align_bytes=64) for c in range(CHUNKS)]
         h_codes = keep.tile([P, J], U32, name="h_codes", align_bytes=64)
         h_scale = keep.tile([P, J], U8, name="h_scale", align_bytes=64)
 
         def round_h(n):
-            c, lo, width = pieces[n]
-            interleave(nc.scalar.copy if c < ON_SCALAR else nc.vector.tensor_copy, h_bf[c][:, PACK * lo : PACK * (lo + width)], h_raw[n][:])
+            c, t0, rows = pieces[n]
+            interleave(nc.scalar.copy if c < ON_SCALAR else nc.vector.tensor_copy, h_bf[c][:], h_raw[n][:], t0)
 
         def quantise_h(c):
             cols = slice(c * W, (c + 1) * W)
@@ -115,7 +119,7 @@ def tile_picked_zdeja_bias_po_kernel(tc, x_words, x_scales, hT, bias, offs, out_
         deal(0, "x_codes0")
         round_h(0)
         quantise_h(0)
-        deal(1, "h_raw0_0")
+        deal(1, "raw0")
         for n in range(1, len(pieces)):
             round_h(n)
         for c in range(1, CHUNKS):
@@ -123,11 +127,12 @@ def tile_picked_zdeja_bias_po_kernel(tc, x_words, x_scales, hT, bias, offs, out_
 
         y_codes = keep.tile([P, J], U32, name="y_codes", align_bytes=64)
         y_scale = keep.tile([P, J], U8, name="y_scale", align_bytes=64)
-        y_bf = keep.tile([P, PACK * J], BF16, name="y_bf", tag=f"bf_{LAST}", align_bytes=64)
         y_rows = out_0.rearrange("(p t) j -> p t j", t=PACK)
         words_out = out_1[0].rearrange("p c r -> p (c r)").bitcast(I32)
+        held = {0: "bf_3"}
 
         stored = 0
+        made = 0
         for g in range(CHUNKS):
             lo, hi = g * W, (g + 1) * W
             cols = slice(lo, hi)
@@ -148,21 +153,20 @@ def tile_picked_zdeja_bias_po_kernel(tc, x_words, x_scales, hT, bias, offs, out_
                     done = slice(t + 1 - STORE_ROWS[g], t + 1)
                     nc.sync.dma_start(out=y_rows[:, done, cols], in_=y[:, done, :])
             width = W // PARTS[g]
-            if g == LAST:
-                for u in range(2):
-                    for b in range(PARTS[g]):
-                        first = lo + b * width
-                        interleave_pair(nc.vector.tensor_copy, y_bf[:, PACK * first : PACK * (first + width)], y[:, :, b * width : (b + 1) * width], u)
-            else:
+            y_bf = []
+            for b in range(PARTS[g]):
+                y_bf.append(keep.tile([P, PACK * width], BF16, name=f"y_bf{made}", tag=held.get(made, f"y_bf{made}"), align_bytes=64))
+                made = made + 1
+            row_sets = ((0, 2), (2, 2)) if g == CHUNKS else ((0, PACK),)
+            for t0, rows in row_sets:
                 for b in range(PARTS[g]):
-                    first = lo + b * width
-                    interleave(nc.vector.tensor_copy, y_bf[:, PACK * first : PACK * (first + width)], y[:, :, b * width : (b + 1) * width])
+                    interleave(nc.vector.tensor_copy, y_bf[b][:], y[:, t0 : t0 + rows, b * width : (b + 1) * width], t0)
             for b in range(PARTS[g]):
                 first = lo + b * width
                 nc.vector.quantize_mx(
                     out=y_codes[:, first : first + width].bitcast(FP8X4),
                     scales=y_scale[:, first : first + width],
-                    in_=y_bf[:, PACK * first : PACK * (first + width)],
+                    in_=y_bf[b][:],
                 )
             if g in WORDS_AFTER:
                 nc.sync.dma_start(out=words_out[:, stored:hi], in_=y_codes[:, stored:hi].bitcast(I32))

@@ -61,9 +61,9 @@ def tile_picked_zdeja_bias_po_kernel(tc, x_words, x_scales, hT, bias, offs, out_
         def load_h(c, tag):
             raw = keep.tile([P, PACK, W], F32, name=f"h_raw{c}", tag=tag, align_bytes=64)
             nc.sync.dma_start(out=raw[:], in_=h_rows[:, :, c * W : (c + 1) * W])
-            h_raw.append(raw)
+            h_raw.append(raw[:])
 
-        for c in range(3):
+        for c in range(2):
             load_h(c, f"raw{c}")
 
         x_scale = keep.tile([P, S], U8, name="x_scale", align_bytes=64)
@@ -90,15 +90,18 @@ def tile_picked_zdeja_bias_po_kernel(tc, x_words, x_scales, hT, bias, offs, out_
                 out=x_scale[r:P:32, :].bitcast(I32),
                 in_=dealt_scales[ROW0 + r : ROW0 + 16 : 4, :].bitcast(I32),
             )
-        for c in range(3, CHUNKS):
-            load_h(c, f"picked{CHUNKS - c}" if c < LAST else "picked1")
+        late = keep.tile([P, 2 * PACK, W], F32, name="h_late", tag="picked1", align_bytes=64)
+        for c in range(2, CHUNKS):
+            raw = late[:, PACK * (c - 2) : PACK * (c - 1), :]
+            nc.sync.dma_start(out=raw, in_=h_rows[:, :, c * W : (c + 1) * W])
+            h_raw.append(raw)
         h_bf = [keep.tile([P, PACK * W], BF16, name=f"h_bf{c}", tag=f"bf_{c}", align_bytes=64) for c in range(CHUNKS)]
         h_codes = keep.tile([P, J], U32, name="h_codes", align_bytes=64)
         h_scale = keep.tile([P, J], U8, name="h_scale", align_bytes=64)
 
         def round_h(n):
             c, t0, rows = pieces[n]
-            interleave(nc.scalar.copy if c < ON_SCALAR else nc.vector.tensor_copy, h_bf[c][:], h_raw[n][:], t0)
+            interleave(nc.scalar.copy if c < ON_SCALAR else nc.vector.tensor_copy, h_bf[c][:], h_raw[n], t0)
 
         def quantise_h(c):
             cols = slice(c * W, (c + 1) * W)

@@ -86,7 +86,8 @@ def tile_picked_zdeja_bias_po_kernel(tc, x_words, x_scales, hT, bias, offs, out_
                 in_=picked_scales[a][:].rearrange("p (m t) -> p t m", t=PACK),
             )
         for r in range(4):
-            nc.sync.dma_start(
+            queue = nc.sync if r % 2 == 0 else nc.scalar
+            queue.dma_start(
                 out=x_scale[r:P:32, :].bitcast(I32),
                 in_=dealt_scales[ROW0 + r : ROW0 + 16 : 4, :].bitcast(I32),
             )
@@ -107,22 +108,14 @@ def tile_picked_zdeja_bias_po_kernel(tc, x_words, x_scales, hT, bias, offs, out_
             cols = slice(c * W, (c + 1) * W)
             nc.vector.quantize_mx(out=h_codes[:, cols].bitcast(FP8X4), scales=h_scale[:, cols], in_=h_bf[c][:])
 
-        picked_words = keep.tile([P, S], U32, name="picked_words", align_bytes=64)
-        nc.vector.tensor_copy(out=picked_words[:], in_=table_words[:].indirect(offsets[:]))
-        x_codes = []
-
-        def deal(u, tag):
-            dealt = keep.tile([P, 2 * P], U32, name=f"x_codes{u}", tag=tag, align_bytes=64)
-            nc.vector.tensor_copy(
-                out=dealt[:].rearrange("p (t c i) -> p c t i", t=2, i=4),
-                in_=picked_words[:].rearrange("p (c i t) -> p c t i", t=PACK, i=4)[:, :, 2 * u : 2 * u + 2, :],
-            )
-            x_codes.extend([dealt[:, :P], dealt[:, P:]])
-
-        deal(0, "x_codes0")
+        dealt_words = keep.tile([P, S], U32, name="dealt_words", align_bytes=64)
+        nc.vector.tensor_copy(
+            out=dealt_words[:].rearrange("p (t m) -> p m t", t=PACK),
+            in_=table_words[:].indirect(offsets[:]),
+        )
+        x_codes = [dealt_words[:, t * P : (t + 1) * P] for t in range(PACK)]
         round_h(0)
         quantise_h(0)
-        deal(1, "raw0")
         for n in range(1, len(pieces)):
             round_h(n)
         for c in range(1, CHUNKS):
@@ -132,10 +125,9 @@ def tile_picked_zdeja_bias_po_kernel(tc, x_words, x_scales, hT, bias, offs, out_
         y_scale = keep.tile([P, J], U8, name="y_scale", align_bytes=64)
         y_rows = out_0.rearrange("(p t) j -> p t j", t=PACK)
         words_out = out_1[0].rearrange("p c r -> p (c r)").bitcast(I32)
-        held = {0: "bf_3"}
+        y_rounded = keep.tile([P, PACK * J], BF16, name="y_rounded", tag="bf_3", align_bytes=64)
 
         stored = 0
-        made = 0
         for g in range(CHUNKS):
             lo, hi = g * W, (g + 1) * W
             cols = slice(lo, hi)
@@ -156,20 +148,15 @@ def tile_picked_zdeja_bias_po_kernel(tc, x_words, x_scales, hT, bias, offs, out_
                     done = slice(t + 1 - STORE_ROWS[g], t + 1)
                     nc.sync.dma_start(out=y_rows[:, done, cols], in_=y[:, done, :])
             width = W // PARTS[g]
-            y_bf = []
+            y_bf = [y_rounded[:, PACK * (lo + b * width) : PACK * (lo + (b + 1) * width)] for b in range(PARTS[g])]
             for b in range(PARTS[g]):
-                y_bf.append(keep.tile([P, PACK * width], BF16, name=f"y_bf{made}", tag=held.get(made, f"y_bf{made}"), align_bytes=64))
-                made = made + 1
-            row_sets = ((0, 2), (2, 2)) if g == CHUNKS else ((0, PACK),)
-            for t0, rows in row_sets:
-                for b in range(PARTS[g]):
-                    interleave(nc.vector.tensor_copy, y_bf[b][:], y[:, t0 : t0 + rows, b * width : (b + 1) * width], t0)
+                interleave(nc.vector.tensor_copy, y_bf[b], y[:, :, b * width : (b + 1) * width])
             for b in range(PARTS[g]):
                 first = lo + b * width
                 nc.vector.quantize_mx(
                     out=y_codes[:, first : first + width].bitcast(FP8X4),
                     scales=y_scale[:, first : first + width],
-                    in_=y_bf[b][:],
+                    in_=y_bf[b],
                 )
             if g in WORDS_AFTER:
                 nc.sync.dma_start(out=words_out[:, stored:hi], in_=y_codes[:, stored:hi].bitcast(I32))

@@ -125,7 +125,7 @@ def tile_picked_zdeja_bias_po_kernel(tc, x_words, x_scales, hT, bias, offs, out_
         y_scale = keep.tile([P, J], U8, name="y_scale", align_bytes=64)
         y_rows = out_0.rearrange("(p t) j -> p t j", t=PACK)
         words_out = out_1[0].rearrange("p c r -> p (c r)").bitcast(I32)
-        y_rounded = keep.tile([P, PACK * J], BF16, name="y_rounded", tag="bf_3", align_bytes=64)
+        y_rounded = keep.tile([P, PACK * J], BF16, name="y_rounded", tag="bf_2", align_bytes=64)
 
         stored = 0
         for g in range(CHUNKS):

@@ -21,7 +21,7 @@ CHUNKS = J // W
 LAST = CHUNKS - 1
 HEAD = 128
 ROW0 = 48
-ON_SCALAR = 2
+ON_SCALAR = 1
 HALVES = 2
 STORE_ROWS = (2,4,4,4)
 PARTS = (1,1,1,2)
@@ -96,7 +96,7 @@ def tile_picked_zdeja_bias_po_kernel(tc, x_words, x_scales, hT, bias, offs, out_
             raw = late[:, PACK * (c - 2) : PACK * (c - 1), :]
             nc.sync.dma_start(out=raw, in_=h_rows[:, :, c * W : (c + 1) * W])
             h_raw.append(raw)
-        h_bf = [keep.tile([P, PACK * W], BF16, name=f"h_bf{c}", tag=f"bf_{c}", align_bytes=64) for c in range(CHUNKS)]
+        h_bf = [keep.tile([P, PACK * W], BF16, name=f"h_bf{c}", tag="raw0" if c == 1 else f"bf_{c}", align_bytes=64) for c in range(CHUNKS)]
         h_codes = keep.tile([P, J], U32, name="h_codes", align_bytes=64)
         h_scale = keep.tile([P, J], U8, name="h_scale", align_bytes=64)
 

@@ -44,15 +44,13 @@ def tile_picked_zdeja_bias_po_kernel(tc, x_words, x_scales, hT, bias, offs, out_
 
         table_words = keep.tile([P, T], U32, name="table_words", align_bytes=64)
         words_in = x_words[0].rearrange("p c r -> p (c r)").bitcast(I32)
-        nc.sync.dma_start(out=table_words[:, :HEAD].bitcast(I32), in_=words_in[:, :HEAD])
         table_scales = keep.tile([P, T], U8, name="table_scales", align_bytes=64)
         nc.sync.dma_start(out=table_scales[ROW0 : ROW0 + 16, :].bitcast(I32), in_=x_scales[0].bitcast(I32))
         offsets = keep.tile([P, S // 16], U16, name="offsets")
         nc.sync.dma_start(offsets[:], offs)
+        nc.sync.dma_start(out=table_words[:, :HEAD].bitcast(I32), in_=words_in[:, :HEAD])
         nc.vector.memset(table_scales[:ROW0, :].bitcast(I32), 0)
         nc.vector.memset(table_scales[ROW0 + 16 :, :].bitcast(I32), 0)
-        bias_sb = keep.tile([P, PACK], F32, name="bias_sb")
-        nc.gpsimd.dma_start(out=bias_sb[:], in_=bias.rearrange("(p t) o -> p (t o)", t=PACK))
         nc.sync.dma_start(out=table_words[:, HEAD:].bitcast(I32), in_=words_in[:, HEAD:])
         h_rows = hT.rearrange("(p t) j -> p t j", t=PACK)
         pieces = [(c, 0, PACK) for c in range(CHUNKS)]
@@ -91,9 +89,11 @@ def tile_picked_zdeja_bias_po_kernel(tc, x_words, x_scales, hT, bias, offs, out_
                 out=x_scale[r:P:32, :].bitcast(I32),
                 in_=dealt_scales[ROW0 + r : ROW0 + 16 : 4, :].bitcast(I32),
             )
-        late = keep.tile([P, 2 * PACK, W], F32, name="h_late", tag="picked1", align_bytes=64)
+        late = keep.tile([P, 2 * PACK * W + PACK], F32, name="late", tag="picked1", align_bytes=64)
+        bias_sb = late[:, 2 * PACK * W :]
+        nc.sync.dma_start(out=bias_sb, in_=bias.rearrange("(p t) o -> p (t o)", t=PACK))
         for c in range(2, CHUNKS):
-            raw = late[:, PACK * (c - 2) : PACK * (c - 1), :]
+            raw = late[:, PACK * W * (c - 2) : PACK * W * (c - 1)].rearrange("p (t j) -> p t j", t=PACK)
             nc.sync.dma_start(out=raw, in_=h_rows[:, :, c * W : (c + 1) * W])
             h_raw.append(raw)
         h_bf = [keep.tile([P, PACK * W], BF16, name=f"h_bf{c}", tag="raw0" if c == 1 else f"bf_{c}", align_bytes=64) for c in range(CHUNKS)]
@@ -125,7 +125,7 @@ def tile_picked_zdeja_bias_po_kernel(tc, x_words, x_scales, hT, bias, offs, out_
         y_scale = keep.tile([P, J], U8, name="y_scale", align_bytes=64)
         y_rows = out_0.rearrange("(p t) j -> p t j", t=PACK)
         words_out = out_1[0].rearrange("p c r -> p (c r)").bitcast(I32)
-        y_rounded = keep.tile([P, PACK * J], BF16, name="y_rounded", tag="bf_2", align_bytes=64)
+        y_rounded = keep.tile([P, PACK * J], BF16, name="y_rounded", tag="bf_3", align_bytes=64)
 
         stored = 0
         for g in range(CHUNKS):

@@ -18,20 +18,19 @@ P = 128
 PACK = 4
 W = 128
 CHUNKS = J // W
-LAST = CHUNKS - 1
 HEAD = 128
 ROW0 = 48
-ON_SCALAR = 1
 HALVES = 2
-STORE_ROWS = (2,4,4,4)
-PARTS = (1,1,1,2)
-WORDS_AFTER = (1,3,)
+ON_SCALAR = 1
+EARLY = 2
+STORE_ROWS = (2, 4, 4, 4)
+PARTS = (1, 1, 1, 2)
+WORDS_AFTER = (2, 3)
 
 
-def interleave(copy, dst, src, t0=0):
-    rows = src.shape[1]
+def interleave(copy, dst, src):
     copy(
-        out=dst.rearrange("p (c i t) -> p c t i", i=4, t=PACK)[:, :, t0 : t0 + rows, :],
+        out=dst.rearrange("p (c i t) -> p c t i", i=4, t=PACK),
         in_=src.rearrange("p t (c i) -> p c t i", i=4),
     )
 
@@ -42,27 +41,22 @@ def tile_picked_zdeja_bias_po_kernel(tc, x_words, x_scales, hT, bias, offs, out_
         keep = ctx.enter_context(tc.tile_pool(name="keep", bufs=1))
         psum = ctx.enter_context(tc.psum_pool(name="psum", bufs=1))
 
-        table_words = keep.tile([P, T], U32, name="table_words", align_bytes=64)
-        words_in = x_words[0].rearrange("p c r -> p (c r)").bitcast(I32)
         table_scales = keep.tile([P, T], U8, name="table_scales", align_bytes=64)
-        nc.sync.dma_start(out=table_scales[ROW0 : ROW0 + 16, :].bitcast(I32), in_=x_scales[0].bitcast(I32))
+        nc.scalar.dma_start(out=table_scales[ROW0 : ROW0 + 16, :].bitcast(I32), in_=x_scales[0].bitcast(I32))
         offsets = keep.tile([P, S // 16], U16, name="offsets")
         nc.sync.dma_start(offsets[:], offs)
+        table_words = keep.tile([P, T], U32, name="table_words", align_bytes=64)
+        words_in = x_words[0].rearrange("p c r -> p (c r)").bitcast(I32)
         nc.sync.dma_start(out=table_words[:, :HEAD].bitcast(I32), in_=words_in[:, :HEAD])
-        nc.vector.memset(table_scales[:ROW0, :].bitcast(I32), 0)
-        nc.vector.memset(table_scales[ROW0 + 16 :, :].bitcast(I32), 0)
         nc.sync.dma_start(out=table_words[:, HEAD:].bitcast(I32), in_=words_in[:, HEAD:])
         h_rows = hT.rearrange("(p t) j -> p t j", t=PACK)
-        pieces = [(c, 0, PACK) for c in range(CHUNKS)]
         h_raw = []
-
-        def load_h(c, tag):
-            raw = keep.tile([P, PACK, W], F32, name=f"h_raw{c}", tag=tag, align_bytes=64)
+        for c in range(EARLY):
+            raw = keep.tile([P, PACK, W], F32, name=f"h_raw{c}", tag=f"raw{c}", align_bytes=64)
             nc.sync.dma_start(out=raw[:], in_=h_rows[:, :, c * W : (c + 1) * W])
             h_raw.append(raw[:])
-
-        for c in range(2):
-            load_h(c, f"raw{c}")
+        nc.vector.memset(table_scales[:ROW0, :].bitcast(I32), 0)
+        nc.vector.memset(table_scales[ROW0 + 16 :, :].bitcast(I32), 0)
 
         x_scale = keep.tile([P, S], U8, name="x_scale", align_bytes=64)
         nc.vector.memset(x_scale[:].bitcast(I32), 0)
@@ -89,20 +83,20 @@ def tile_picked_zdeja_bias_po_kernel(tc, x_words, x_scales, hT, bias, offs, out_
                 out=x_scale[r:P:32, :].bitcast(I32),
                 in_=dealt_scales[ROW0 + r : ROW0 + 16 : 4, :].bitcast(I32),
             )
-        late = keep.tile([P, 2 * PACK * W + PACK], F32, name="late", tag="picked1", align_bytes=64)
-        bias_sb = late[:, 2 * PACK * W :]
+        late = keep.tile([P, (CHUNKS - EARLY) * PACK * W + PACK], F32, name="late", tag="picked1", align_bytes=64)
+        bias_sb = late[:, (CHUNKS - EARLY) * PACK * W :]
         nc.sync.dma_start(out=bias_sb, in_=bias.rearrange("(p t) o -> p (t o)", t=PACK))
-        for c in range(2, CHUNKS):
-            raw = late[:, PACK * W * (c - 2) : PACK * W * (c - 1)].rearrange("p (t j) -> p t j", t=PACK)
+        for c in range(EARLY, CHUNKS):
+            raw = late[:, PACK * W * (c - EARLY) : PACK * W * (c - EARLY + 1)].rearrange("p (t j) -> p t j", t=PACK)
             nc.sync.dma_start(out=raw, in_=h_rows[:, :, c * W : (c + 1) * W])
             h_raw.append(raw)
+
         h_bf = [keep.tile([P, PACK * W], BF16, name=f"h_bf{c}", tag="raw0" if c == 1 else f"bf_{c}", align_bytes=64) for c in range(CHUNKS)]
         h_codes = keep.tile([P, J], U32, name="h_codes", align_bytes=64)
         h_scale = keep.tile([P, J], U8, name="h_scale", align_bytes=64)
 
-        def round_h(n):
-            c, t0, rows = pieces[n]
-            interleave(nc.scalar.copy if c < ON_SCALAR else nc.vector.tensor_copy, h_bf[c][:], h_raw[n], t0)
+        def round_h(c):
+            interleave(nc.scalar.copy if c < ON_SCALAR else nc.vector.tensor_copy, h_bf[c][:], h_raw[c])
 
         def quantise_h(c):
             cols = slice(c * W, (c + 1) * W)
@@ -113,11 +107,10 @@ def tile_picked_zdeja_bias_po_kernel(tc, x_words, x_scales, hT, bias, offs, out_
             out=dealt_words[:].rearrange("p (t m) -> p m t", t=PACK),
             in_=table_words[:].indirect(offsets[:]),
         )
-        x_codes = [dealt_words[:, t * P : (t + 1) * P] for t in range(PACK)]
         round_h(0)
         quantise_h(0)
-        for n in range(1, len(pieces)):
-            round_h(n)
+        for c in range(1, CHUNKS):
+            round_h(c)
         for c in range(1, CHUNKS):
             quantise_h(c)
 
@@ -136,7 +129,7 @@ def tile_picked_zdeja_bias_po_kernel(tc, x_words, x_scales, hT, bias, offs, out_
                 acc = psum.tile([P, W], F32, name=f"acc{g % 2}_{t}")
                 nc.tensor.matmul_mx(
                     out=acc[:],
-                    lhsT=x_codes[t].bitcast(FP8X4),
+                    lhsT=dealt_words[:, t * P : (t + 1) * P].bitcast(FP8X4),
                     lhsT_scale=x_scale[:, t * P : (t + 1) * P],
                     rhs=h_codes[:, cols].bitcast(FP8X4),
                     rhs_scale=h_scale[:, cols],
@@ -150,12 +143,12 @@ def tile_picked_zdeja_bias_po_kernel(tc, x_words, x_scales, hT, bias, offs, out_
             width = W // PARTS[g]
             y_bf = [y_rounded[:, PACK * (lo + b * width) : PACK * (lo + (b + 1) * width)] for b in range(PARTS[g])]
             for b in range(PARTS[g]):
-                interleave(nc.vector.tensor_copy, y_bf[b], y[:, :, b * width : (b + 1) * width])
+                interleave(nc.scalar.copy if b == 1 else nc.vector.tensor_copy, y_bf[b], y[:, :, b * width : (b + 1) * width])
             for b in range(PARTS[g]):
-                first = lo + b * width
+                start = lo + b * width
                 nc.vector.quantize_mx(
-                    out=y_codes[:, first : first + width].bitcast(FP8X4),
-                    scales=y_scale[:, first : first + width],
+                    out=y_codes[:, start : start + width].bitcast(FP8X4),
+                    scales=y_scale[:, start : start + width],
                     in_=y_bf[b],
                 )
             if g in WORDS_AFTER:

@@ -21,11 +21,15 @@ CHUNKS = J // W
 HEAD = 128
 ROW0 = 48
 HALVES = 2
-ON_SCALAR = 1
+ON_SCALAR = 2
 EARLY = 2
 STORE_ROWS = (2, 4, 4, 4)
 PARTS = (1, 1, 1, 2)
-WORDS_AFTER = (2, 3)
+WORDS_AFTER = (1, 3)
+ROUNDED_AT = 0
+FOURTH_AT = 2048
+THIRD_AT = 4096
+PICKED_AT = (8192, 3968)
 
 
 def interleave(copy, dst, src):
@@ -39,6 +43,7 @@ def tile_picked_zdeja_bias_po_kernel(tc, x_words, x_scales, hT, bias, offs, out_
     nc = tc.nc
     with ExitStack() as ctx:
         keep = ctx.enter_context(tc.tile_pool(name="keep", bufs=1))
+        reuse = ctx.enter_context(tc.tile_pool(name="reuse", bufs=1))
         psum = ctx.enter_context(tc.psum_pool(name="psum", bufs=1))
 
         table_scales = keep.tile([P, T], U8, name="table_scales", align_bytes=64)
@@ -68,7 +73,7 @@ def tile_picked_zdeja_bias_po_kernel(tc, x_words, x_scales, hT, bias, offs, out_
         part = S // HALVES
         picked_scales = []
         for a in range(HALVES):
-            picked = keep.tile([P, part], U8, name=f"picked_scales{a}", tag=f"picked{a}", align_bytes=64)
+            picked = reuse.tile([P, part], U8, name=f"picked_scales{a}", align_bytes=64, offset=PICKED_AT[a])
             nc.vector.tensor_copy(out=picked[:], in_=table_scales[:].indirect(offsets[:, a * part // 16 : (a + 1) * part // 16]))
             picked_scales.append(picked)
         dealt_scales = keep.tile([P, S], U8, name="dealt_scales", align_bytes=64)
@@ -83,15 +88,16 @@ def tile_picked_zdeja_bias_po_kernel(tc, x_words, x_scales, hT, bias, offs, out_
                 out=x_scale[r:P:32, :].bitcast(I32),
                 in_=dealt_scales[ROW0 + r : ROW0 + 16 : 4, :].bitcast(I32),
             )
-        late = keep.tile([P, (CHUNKS - EARLY) * PACK * W + PACK], F32, name="late", tag="picked1", align_bytes=64)
-        bias_sb = late[:, (CHUNKS - EARLY) * PACK * W :]
+        third = reuse.tile([P, PACK * W + PACK], F32, name="third", align_bytes=64, offset=THIRD_AT)
+        fourth = reuse.tile([P, PACK * W], F32, name="fourth", align_bytes=64, offset=FOURTH_AT)
+        bias_sb = third[:, PACK * W :]
         nc.sync.dma_start(out=bias_sb, in_=bias.rearrange("(p t) o -> p (t o)", t=PACK))
-        for c in range(EARLY, CHUNKS):
-            raw = late[:, PACK * W * (c - EARLY) : PACK * W * (c - EARLY + 1)].rearrange("p (t j) -> p t j", t=PACK)
+        for c, late in ((2, third), (3, fourth)):
+            raw = late[:, : PACK * W].rearrange("p (t j) -> p t j", t=PACK)
             nc.sync.dma_start(out=raw, in_=h_rows[:, :, c * W : (c + 1) * W])
             h_raw.append(raw)
 
-        h_bf = [keep.tile([P, PACK * W], BF16, name=f"h_bf{c}", tag="raw0" if c == 1 else f"bf_{c}", align_bytes=64) for c in range(CHUNKS)]
+        h_bf = [keep.tile([P, PACK * W], BF16, name=f"h_bf{c}", tag=f"bf_{c}", align_bytes=64) for c in range(CHUNKS)]
         h_codes = keep.tile([P, J], U32, name="h_codes", align_bytes=64)
         h_scale = keep.tile([P, J], U8, name="h_scale", align_bytes=64)
 
@@ -111,14 +117,13 @@ def tile_picked_zdeja_bias_po_kernel(tc, x_words, x_scales, hT, bias, offs, out_
         quantise_h(0)
         for c in range(1, CHUNKS):
             round_h(c)
-        for c in range(1, CHUNKS):
             quantise_h(c)
 
         y_codes = keep.tile([P, J], U32, name="y_codes", align_bytes=64)
         y_scale = keep.tile([P, J], U8, name="y_scale", align_bytes=64)
         y_rows = out_0.rearrange("(p t) j -> p t j", t=PACK)
         words_out = out_1[0].rearrange("p c r -> p (c r)").bitcast(I32)
-        y_rounded = keep.tile([P, PACK * J], BF16, name="y_rounded", tag="bf_3", align_bytes=64)
+        y_rounded = reuse.tile([P, PACK * J], BF16, name="y_rounded", align_bytes=64, offset=ROUNDED_AT)
 
         stored = 0
         for g in range(CHUNKS):

@@ -20,7 +20,6 @@ W = 128
 CHUNKS = J // W
 HEAD = 128
 ROW0 = 48
-HALVES = 2
 ON_SCALAR = 2
 EARLY = 2
 STORE_ROWS = (2, 4, 4, 4)
@@ -29,7 +28,8 @@ WORDS_AFTER = (1, 3)
 ROUNDED_AT = 0
 FOURTH_AT = 2048
 THIRD_AT = 4096
-PICKED_AT = (8192, 3968)
+LAST_BF_AT = 5120
+WINDOW_AT = 3072
 
 
 def interleave(copy, dst, src):
@@ -46,10 +46,12 @@ def tile_picked_zdeja_bias_po_kernel(tc, x_words, x_scales, hT, bias, offs, out_
         reuse = ctx.enter_context(tc.tile_pool(name="reuse", bufs=1))
         psum = ctx.enter_context(tc.psum_pool(name="psum", bufs=1))
 
-        table_scales = keep.tile([P, T], U8, name="table_scales", align_bytes=64)
+        table_scales = reuse.tile([P, T], U8, name="table_scales", align_bytes=64, offset=WINDOW_AT)
         nc.scalar.dma_start(out=table_scales[ROW0 : ROW0 + 16, :].bitcast(I32), in_=x_scales[0].bitcast(I32))
         offsets = keep.tile([P, S // 16], U16, name="offsets")
         nc.sync.dma_start(offsets[:], offs)
+        bias_sb = keep.tile([P, PACK], F32, name="bias_sb", align_bytes=64)
+        nc.scalar.dma_start(out=bias_sb[:], in_=bias.rearrange("(p t) o -> p (t o)", t=PACK))
         table_words = keep.tile([P, T], U32, name="table_words", align_bytes=64)
         words_in = x_words[0].rearrange("p c r -> p (c r)").bitcast(I32)
         nc.sync.dma_start(out=table_words[:, :HEAD].bitcast(I32), in_=words_in[:, :HEAD])
@@ -70,34 +72,26 @@ def tile_picked_zdeja_bias_po_kernel(tc, x_words, x_scales, hT, bias, offs, out_
         warm = keep.tile([P, 1], F32, name="warm")
         nc.scalar.activation(out=warm[:], in_=zero[:], func=GELU)
 
-        part = S // HALVES
-        picked_scales = []
-        for a in range(HALVES):
-            picked = reuse.tile([P, part], U8, name=f"picked_scales{a}", align_bytes=64, offset=PICKED_AT[a])
-            nc.vector.tensor_copy(out=picked[:], in_=table_scales[:].indirect(offsets[:, a * part // 16 : (a + 1) * part // 16]))
-            picked_scales.append(picked)
         dealt_scales = keep.tile([P, S], U8, name="dealt_scales", align_bytes=64)
-        for a in range(HALVES):
-            nc.vector.tensor_copy(
-                out=dealt_scales[:].rearrange("p (t m) -> p t m", t=PACK)[:, :, a * part // PACK : (a + 1) * part // PACK],
-                in_=picked_scales[a][:].rearrange("p (m t) -> p t m", t=PACK),
-            )
+        nc.vector.tensor_copy(
+            out=dealt_scales[:].rearrange("p (t m) -> p m t", t=PACK),
+            in_=table_scales[:].indirect(offsets[:]),
+        )
         for r in range(4):
             queue = nc.sync if r % 2 == 0 else nc.scalar
             queue.dma_start(
                 out=x_scale[r:P:32, :].bitcast(I32),
                 in_=dealt_scales[ROW0 + r : ROW0 + 16 : 4, :].bitcast(I32),
             )
-        third = reuse.tile([P, PACK * W + PACK], F32, name="third", align_bytes=64, offset=THIRD_AT)
+        third = reuse.tile([P, PACK * W], F32, name="third", align_bytes=64, offset=THIRD_AT)
         fourth = reuse.tile([P, PACK * W], F32, name="fourth", align_bytes=64, offset=FOURTH_AT)
-        bias_sb = third[:, PACK * W :]
-        nc.sync.dma_start(out=bias_sb, in_=bias.rearrange("(p t) o -> p (t o)", t=PACK))
         for c, late in ((2, third), (3, fourth)):
-            raw = late[:, : PACK * W].rearrange("p (t j) -> p t j", t=PACK)
+            raw = late[:].rearrange("p (t j) -> p t j", t=PACK)
             nc.sync.dma_start(out=raw, in_=h_rows[:, :, c * W : (c + 1) * W])
             h_raw.append(raw)
 
-        h_bf = [keep.tile([P, PACK * W], BF16, name=f"h_bf{c}", tag=f"bf_{c}", align_bytes=64) for c in range(CHUNKS)]
+        h_bf = [keep.tile([P, PACK * W], BF16, name=f"h_bf{c}", tag=tag, align_bytes=64) for c, tag in enumerate(("bf0", "bf1", "raw1"))]
+        h_bf.append(reuse.tile([P, PACK * W], BF16, name="h_bf3", align_bytes=64, offset=LAST_BF_AT))
         h_codes = keep.tile([P, J], U32, name="h_codes", align_bytes=64)
         h_scale = keep.tile([P, J], U8, name="h_scale", align_bytes=64)
 

@@ -18,8 +18,8 @@ P = 128
 PACK = 4
 W = 128
 CHUNKS = J // W
-HEAD = 128
-ROW0 = 48
+HEAD = 256
+ROW0 = 112
 ON_SCALAR = 2
 EARLY = 2
 STORE_ROWS = (2, 4, 4, 4)
@@ -50,11 +50,11 @@ def tile_picked_zdeja_bias_po_kernel(tc, x_words, x_scales, hT, bias, offs, out_
         nc.scalar.dma_start(out=table_scales[ROW0 : ROW0 + 16, :].bitcast(I32), in_=x_scales[0].bitcast(I32))
         offsets = keep.tile([P, S // 16], U16, name="offsets")
         nc.sync.dma_start(offsets[:], offs)
-        bias_sb = keep.tile([P, PACK], F32, name="bias_sb", align_bytes=64)
-        nc.scalar.dma_start(out=bias_sb[:], in_=bias.rearrange("(p t) o -> p (t o)", t=PACK))
         table_words = keep.tile([P, T], U32, name="table_words", align_bytes=64)
         words_in = x_words[0].rearrange("p c r -> p (c r)").bitcast(I32)
         nc.sync.dma_start(out=table_words[:, :HEAD].bitcast(I32), in_=words_in[:, :HEAD])
+        bias_rows = keep.tile([P, P], F32, name="bias_rows", align_bytes=64)
+        nc.sync.dma_start(out=bias_rows[31:P:32, :], in_=bias.rearrange("(q i) o -> q (i o)", q=4))
         nc.sync.dma_start(out=table_words[:, HEAD:].bitcast(I32), in_=words_in[:, HEAD:])
         h_rows = hT.rearrange("(p t) j -> p t j", t=PACK)
         h_raw = []
@@ -63,8 +63,9 @@ def tile_picked_zdeja_bias_po_kernel(tc, x_words, x_scales, hT, bias, offs, out_
             nc.sync.dma_start(out=raw[:], in_=h_rows[:, :, c * W : (c + 1) * W])
             h_raw.append(raw[:])
         nc.vector.memset(table_scales[:ROW0, :].bitcast(I32), 0)
-        nc.vector.memset(table_scales[ROW0 + 16 :, :].bitcast(I32), 0)
 
+        for q in range(4):
+            nc.vector.memset(bias_rows[32 * q : 32 * q + 31, :], 0.0)
         x_scale = keep.tile([P, S], U8, name="x_scale", align_bytes=64)
         nc.vector.memset(x_scale[:].bitcast(I32), 0)
         zero = keep.tile([P, 1], F32, name="zero")
@@ -83,6 +84,11 @@ def tile_picked_zdeja_bias_po_kernel(tc, x_words, x_scales, hT, bias, offs, out_
                 out=x_scale[r:P:32, :].bitcast(I32),
                 in_=dealt_scales[ROW0 + r : ROW0 + 16 : 4, :].bitcast(I32),
             )
+        bias_sorted = keep.tile([P, P], F32, name="bias_sorted", align_bytes=64)
+        nc.scalar.copy(
+            out=bias_sorted[:].rearrange("p (t i) -> p t i", t=PACK),
+            in_=bias_rows[:].rearrange("p (i t) -> p t i", t=PACK),
+        )
         third = reuse.tile([P, PACK * W], F32, name="third", align_bytes=64, offset=THIRD_AT)
         fourth = reuse.tile([P, PACK * W], F32, name="fourth", align_bytes=64, offset=FOURTH_AT)
         for c, late in ((2, third), (3, fourth)):
@@ -109,6 +115,8 @@ def tile_picked_zdeja_bias_po_kernel(tc, x_words, x_scales, hT, bias, offs, out_
         )
         round_h(0)
         quantise_h(0)
+        bias_turned = keep.tile([P, P], F32, name="bias_turned", tag="raw0", align_bytes=64)
+        nc.vector.transpose(bias_turned[:], bias_sorted[:])
         for c in range(1, CHUNKS):
             round_h(c)
             quantise_h(c)
@@ -135,7 +143,7 @@ def tile_picked_zdeja_bias_po_kernel(tc, x_words, x_scales, hT, bias, offs, out_
                     start=True,
                     stop=True,
                 )
-                nc.scalar.activation(out=y[:, t, :], in_=acc[:], func=GELU, bias=bias_sb[:, t : t + 1])
+                nc.scalar.activation(out=y[:, t, :], in_=acc[:], func=GELU, bias=bias_turned[:, 32 * t + 31 : 32 * t + 32])
                 if (t + 1) % STORE_ROWS[g] == 0:
                     done = slice(t + 1 - STORE_ROWS[g], t + 1)
                     nc.sync.dma_start(out=y_rows[:, done, cols], in_=y[:, done, :])

@@ -17,8 +17,9 @@ GELU = mybir.ActivationFunctionType.Gelu_apprx_tanh
 P = 128
 PACK = 4
 W = 128
+HALF = W // 2
 CHUNKS = J // W
-HEAD = 256
+HEAD = 128
 ROW0 = 112
 ON_SCALAR = 2
 EARLY = 2
@@ -48,13 +49,13 @@ def tile_picked_zdeja_bias_po_kernel(tc, x_words, x_scales, hT, bias, offs, out_
 
         table_scales = reuse.tile([P, T], U8, name="table_scales", align_bytes=64, offset=WINDOW_AT)
         nc.scalar.dma_start(out=table_scales[ROW0 : ROW0 + 16, :].bitcast(I32), in_=x_scales[0].bitcast(I32))
-        offsets = keep.tile([P, S // 16], U16, name="offsets")
-        nc.sync.dma_start(offsets[:], offs)
         table_words = keep.tile([P, T], U32, name="table_words", align_bytes=64)
         words_in = x_words[0].rearrange("p c r -> p (c r)").bitcast(I32)
         nc.sync.dma_start(out=table_words[:, :HEAD].bitcast(I32), in_=words_in[:, :HEAD])
+        offsets = keep.tile([P, S // 16], U16, name="offsets")
+        nc.sync.dma_start(offsets[:], offs)
         bias_rows = keep.tile([P, P], F32, name="bias_rows", align_bytes=64)
-        nc.sync.dma_start(out=bias_rows[31:P:32, :], in_=bias.rearrange("(q i) o -> q (i o)", q=4))
+        nc.scalar.dma_start(out=bias_rows[31:P:32, :], in_=bias.rearrange("(q i) o -> q (i o)", q=4))
         nc.sync.dma_start(out=table_words[:, HEAD:].bitcast(I32), in_=words_in[:, HEAD:])
         h_rows = hT.rearrange("(p t) j -> p t j", t=PACK)
         h_raw = []
@@ -101,25 +102,30 @@ def tile_picked_zdeja_bias_po_kernel(tc, x_words, x_scales, hT, bias, offs, out_
         h_codes = keep.tile([P, J], U32, name="h_codes", align_bytes=64)
         h_scale = keep.tile([P, J], U8, name="h_scale", align_bytes=64)
 
-        def round_h(c):
-            interleave(nc.scalar.copy if c < ON_SCALAR else nc.vector.tensor_copy, h_bf[c][:], h_raw[c])
+        def round_h(c, a, b):
+            copy = nc.scalar.copy if c < ON_SCALAR else nc.vector.tensor_copy
+            interleave(copy, h_bf[c][:, PACK * a : PACK * b], h_raw[c][:, :, a:b])
 
-        def quantise_h(c):
-            cols = slice(c * W, (c + 1) * W)
-            nc.vector.quantize_mx(out=h_codes[:, cols].bitcast(FP8X4), scales=h_scale[:, cols], in_=h_bf[c][:])
+        def quantise_h(c, a, b):
+            cols = slice(c * W + a, c * W + b)
+            nc.vector.quantize_mx(out=h_codes[:, cols].bitcast(FP8X4), scales=h_scale[:, cols], in_=h_bf[c][:, PACK * a : PACK * b])
 
         dealt_words = keep.tile([P, S], U32, name="dealt_words", align_bytes=64)
         nc.vector.tensor_copy(
             out=dealt_words[:].rearrange("p (t m) -> p m t", t=PACK),
             in_=table_words[:].indirect(offsets[:]),
         )
-        round_h(0)
-        quantise_h(0)
+        round_h(0, 0, W)
+        quantise_h(0, 0, W)
         bias_turned = keep.tile([P, P], F32, name="bias_turned", tag="raw0", align_bytes=64)
         nc.vector.transpose(bias_turned[:], bias_sorted[:])
-        for c in range(1, CHUNKS):
-            round_h(c)
-            quantise_h(c)
+        round_h(1, 0, W)
+        quantise_h(1, 0, W)
+        for c in range(ON_SCALAR, CHUNKS):
+            for a in (0, HALF):
+                round_h(c, a, a + HALF)
+            for a in (0, HALF):
+                quantise_h(c, a, a + HALF)
 
         y_codes = keep.tile([P, J], U32, name="y_codes", align_bytes=64)
         y_scale = keep.tile([P, J], U8, name="y_scale", align_bytes=64)

@@ -23,9 +23,7 @@ HEAD = 128
 ROW0 = 112
 ON_SCALAR = 2
 EARLY = 2
-STORE_ROWS = (2, 4, 4, 4)
-PARTS = (1, 1, 1, 2)
-WORDS_AFTER = (1, 3)
+BANKS = 8
 ROUNDED_AT = 0
 FOURTH_AT = 2048
 THIRD_AT = 4096
@@ -133,40 +131,52 @@ def tile_picked_zdeja_bias_po_kernel(tc, x_words, x_scales, hT, bias, offs, out_
         words_out = out_1[0].rearrange("p c r -> p (c r)").bitcast(I32)
         y_rounded = reuse.tile([P, PACK * J], BF16, name="y_rounded", align_bytes=64, offset=ROUNDED_AT)
 
-        stored = 0
-        for g in range(CHUNKS):
-            lo, hi = g * W, (g + 1) * W
-            cols = slice(lo, hi)
-            y = keep.tile([P, PACK, W], F32, name=f"y{g}", align_bytes=64)
-            for t in range(PACK):
-                acc = psum.tile([P, W], F32, name=f"acc{g % 2}_{t}")
-                nc.tensor.matmul_mx(
-                    out=acc[:],
-                    lhsT=dealt_words[:, t * P : (t + 1) * P].bitcast(FP8X4),
-                    lhsT_scale=x_scale[:, t * P : (t + 1) * P],
-                    rhs=h_codes[:, cols].bitcast(FP8X4),
-                    rhs_scale=h_scale[:, cols],
-                    start=True,
-                    stop=True,
-                )
-                nc.scalar.activation(out=y[:, t, :], in_=acc[:], func=GELU, bias=bias_turned[:, 32 * t + 31 : 32 * t + 32])
-                if (t + 1) % STORE_ROWS[g] == 0:
-                    done = slice(t + 1 - STORE_ROWS[g], t + 1)
-                    nc.sync.dma_start(out=y_rows[:, done, cols], in_=y[:, done, :])
-            width = W // PARTS[g]
-            y_bf = [y_rounded[:, PACK * (lo + b * width) : PACK * (lo + (b + 1) * width)] for b in range(PARTS[g])]
-            for b in range(PARTS[g]):
-                interleave(nc.scalar.copy if b == 1 else nc.vector.tensor_copy, y_bf[b], y[:, :, b * width : (b + 1) * width])
-            for b in range(PARTS[g]):
-                start = lo + b * width
-                nc.vector.quantize_mx(
-                    out=y_codes[:, start : start + width].bitcast(FP8X4),
-                    scales=y_scale[:, start : start + width],
-                    in_=y_bf[b],
-                )
-            if g in WORDS_AFTER:
-                nc.sync.dma_start(out=words_out[:, stored:hi], in_=y_codes[:, stored:hi].bitcast(I32))
-                stored = hi
+        y = keep.tile([P, PACK, J], F32, name="y", align_bytes=64)
+
+        def product(t, lo, hi, bank):
+            acc = psum.tile([P, hi - lo], F32, name=f"acc{bank}", tag=f"bank{bank % BANKS}")
+            nc.tensor.matmul_mx(
+                out=acc[:],
+                lhsT=dealt_words[:, t * P : (t + 1) * P].bitcast(FP8X4),
+                lhsT_scale=x_scale[:, t * P : (t + 1) * P],
+                rhs=h_codes[:, lo:hi].bitcast(FP8X4),
+                rhs_scale=h_scale[:, lo:hi],
+                start=True,
+                stop=True,
+            )
+            nc.scalar.activation(out=y[:, t, lo:hi], in_=acc[:], func=GELU, bias=bias_turned[:, 32 * t + 31 : 32 * t + 32])
+
+        def round_y(copy, lo, hi):
+            interleave(copy, y_rounded[:, PACK * lo : PACK * hi], y[:, :, lo:hi])
+
+        def quantise_y(lo, hi):
+            nc.vector.quantize_mx(out=y_codes[:, lo:hi].bitcast(FP8X4), scales=y_scale[:, lo:hi], in_=y_rounded[:, PACK * lo : PACK * hi])
+
+        def store_words(lo, hi):
+            nc.sync.dma_start(out=words_out[:, lo:hi], in_=y_codes[:, lo:hi].bitcast(I32))
+
+        bank = 0
+        for step in range(CHUNKS + 1):
+            first_row = 2 if step % 2 == 0 else 0
+            lo, hi = max(step - 1, 0) * W, min(step + 1, CHUNKS) * W
+            for a in range(lo, hi, W):
+                for t in (first_row, first_row + 1):
+                    product(t, a, a + W, bank)
+                    bank = bank + 1
+            nc.sync.dma_start(out=y_rows[:, first_row : first_row + 2, lo:hi], in_=y[:, first_row : first_row + 2, lo:hi])
+            if 1 <= step < CHUNKS:
+                round_y(nc.vector.tensor_copy, lo, lo + W)
+            if step == CHUNKS:
+                round_y(nc.vector.tensor_copy, lo, lo + HALF)
+                round_y(nc.scalar.copy, lo + HALF, hi)
+                quantise_y(lo - W, lo)
+                quantise_y(lo, lo + HALF)
+                quantise_y(lo + HALF, hi)
+                store_words(2 * W, hi)
+            elif 1 <= step < CHUNKS - 1:
+                quantise_y(lo, lo + W)
+            if step == 2:
+                store_words(0, 2 * W)
         for q in range(4):
             queue = nc.scalar if q % 2 == 0 else nc.sync
             queue.dma_start(

@@ -47,11 +47,11 @@ def tile_picked_zdeja_bias_po_kernel(tc, x_words, x_scales, hT, bias, offs, out_
 
         table_scales = reuse.tile([P, T], U8, name="table_scales", align_bytes=64, offset=WINDOW_AT)
         nc.scalar.dma_start(out=table_scales[ROW0 : ROW0 + 16, :].bitcast(I32), in_=x_scales[0].bitcast(I32))
+        offsets = keep.tile([P, S // 16], U16, name="offsets")
+        nc.sync.dma_start(offsets[:], offs)
         table_words = keep.tile([P, T], U32, name="table_words", align_bytes=64)
         words_in = x_words[0].rearrange("p c r -> p (c r)").bitcast(I32)
         nc.sync.dma_start(out=table_words[:, :HEAD].bitcast(I32), in_=words_in[:, :HEAD])
-        offsets = keep.tile([P, S // 16], U16, name="offsets")
-        nc.sync.dma_start(offsets[:], offs)
         bias_rows = keep.tile([P, P], F32, name="bias_rows", align_bytes=64)
         nc.scalar.dma_start(out=bias_rows[31:P:32, :], in_=bias.rearrange("(q i) o -> q (i o)", q=4))
         nc.sync.dma_start(out=table_words[:, HEAD:].bitcast(I32), in_=words_in[:, HEAD:])
@@ -109,10 +109,17 @@ def tile_picked_zdeja_bias_po_kernel(tc, x_words, x_scales, hT, bias, offs, out_
             nc.vector.quantize_mx(out=h_codes[:, cols].bitcast(FP8X4), scales=h_scale[:, cols], in_=h_bf[c][:, PACK * a : PACK * b])
 
         dealt_words = keep.tile([P, S], U32, name="dealt_words", align_bytes=64)
-        nc.vector.tensor_copy(
-            out=dealt_words[:].rearrange("p (t m) -> p m t", t=PACK),
-            in_=table_words[:].indirect(offsets[:]),
-        )
+        picked_words = keep.tile([P, S], U32, name="picked_words", align_bytes=64)
+        for half in range(2):
+            nc.vector.tensor_copy(
+                out=picked_words[:, half * S // 2 : (half + 1) * S // 2],
+                in_=table_words[:].indirect(offsets[:, half * S // 32 : (half + 1) * S // 32]),
+            )
+        dealt_view = dealt_words[:].bitcast(I32).rearrange("p (t a i) -> p a t i", t=PACK, i=4)
+        picked_view = picked_words[:].bitcast(I32).rearrange("p (a i t) -> p a t i", t=PACK, i=4)
+        for half in range(2):
+            rows = slice(half * S // 32, (half + 1) * S // 32)
+            nc.vector.tensor_copy(out=dealt_view[:, rows], in_=picked_view[:, rows])
         round_h(0, 0, W)
         quantise_h(0, 0, W)
         bias_turned = keep.tile([P, P], F32, name="bias_turned", tag="raw0", align_bytes=64)

@@ -33,8 +33,8 @@ WINDOW_AT = 3072
 
 def interleave(copy, dst, src):
     copy(
-        out=dst.rearrange("p (c i t) -> p c t i", i=4, t=PACK),
-        in_=src.rearrange("p t (c i) -> p c t i", i=4),
+        out=dst.rearrange("p (c i t) -> p c t i", i=2, t=PACK),
+        in_=src.rearrange("p t (c i) -> p c t i", i=2),
     )
 
 

@@ -123,7 +123,8 @@ def tile_picked_zdeja_bias_po_kernel(tc, x_words, x_scales, hT, bias, offs, out_
         round_h(0, 0, W)
         quantise_h(0, 0, W)
         bias_turned = keep.tile([P, P], F32, name="bias_turned", tag="raw0", align_bytes=64)
-        nc.vector.transpose(bias_turned[:], bias_sorted[:])
+        for t in (2, 3, 0, 1):
+            nc.vector.transpose(bias_turned[:, 32 * t : 32 * t + 32], bias_sorted[:, 32 * t : 32 * t + 32])
         round_h(1, 0, W)
         quantise_h(1, 0, W)
         for c in range(ON_SCALAR, CHUNKS):

from contextlib import ExitStack

import concourse.mybir as mybir

K, T, S, J = 512, 2048, 512, 512
FLOPS = 2 * K * S * J

F32 = mybir.dt.float32
BF16 = mybir.dt.bfloat16
I32 = mybir.dt.int32
U32 = mybir.dt.uint32
U16 = mybir.dt.uint16
U8 = mybir.dt.uint8
FP8X4 = mybir.dt.float8_e4m3fn_x4
GELU = mybir.ActivationFunctionType.Gelu_apprx_tanh

P = 128
PACK = 4
W = 128
HALF = W // 2
CHUNKS = J // W
HEAD = 128
ROW0 = 112
ON_SCALAR = 2
EARLY = 2
BANKS = 8
ROUNDED_AT = 0
FOURTH_AT = 2048
THIRD_AT = 4096
LAST_BF_AT = 5120
WINDOW_AT = 3072


def interleave(copy, dst, src):
    copy(
        out=dst.rearrange("p (c i t) -> p c t i", i=2, t=PACK),
        in_=src.rearrange("p t (c i) -> p c t i", i=2),
    )


def tile_picked_zdeja_bias_po_kernel(tc, x_words, x_scales, hT, bias, offs, out_0, out_1, out_2):
    nc = tc.nc
    with ExitStack() as ctx:
        keep = ctx.enter_context(tc.tile_pool(name="keep", bufs=1))
        reuse = ctx.enter_context(tc.tile_pool(name="reuse", bufs=1))
        psum = ctx.enter_context(tc.psum_pool(name="psum", bufs=1))

        table_scales = reuse.tile([P, T], U8, name="table_scales", align_bytes=64, offset=WINDOW_AT)
        nc.scalar.dma_start(out=table_scales[ROW0 : ROW0 + 16, :].bitcast(I32), in_=x_scales[0].bitcast(I32))
        offsets = keep.tile([P, S // 16], U16, name="offsets")
        nc.sync.dma_start(offsets[:], offs)
        table_words = keep.tile([P, T], U32, name="table_words", align_bytes=64)
        words_in = x_words[0].rearrange("p c r -> p (c r)").bitcast(I32)
        nc.sync.dma_start(out=table_words[:, :HEAD].bitcast(I32), in_=words_in[:, :HEAD])
        bias_rows = keep.tile([P, P], F32, name="bias_rows", align_bytes=64)
        nc.scalar.dma_start(out=bias_rows[31:P:32, :], in_=bias.rearrange("(q i) o -> q (i o)", q=4))
        nc.sync.dma_start(out=table_words[:, HEAD:].bitcast(I32), in_=words_in[:, HEAD:])
        h_rows = hT.rearrange("(p t) j -> p t j", t=PACK)
        h_raw = []
        for c in range(EARLY):
            raw = keep.tile([P, PACK, W], F32, name=f"h_raw{c}", tag=f"raw{c}", align_bytes=64)
            nc.sync.dma_start(out=raw[:], in_=h_rows[:, :, c * W : (c + 1) * W])
            h_raw.append(raw[:])
        nc.vector.memset(table_scales[:ROW0, :].bitcast(I32), 0)

        for q in range(4):
            nc.vector.memset(bias_rows[32 * q : 32 * q + 31, :], 0.0)
        x_scale = keep.tile([P, S], U8, name="x_scale", align_bytes=64)
        nc.vector.memset(x_scale[:].bitcast(I32), 0)
        zero = keep.tile([P, 1], F32, name="zero")
        nc.vector.memset(zero[:], 0.0)
        warm = keep.tile([P, 1], F32, name="warm")
        nc.scalar.activation(out=warm[:], in_=zero[:], func=GELU)

        dealt_scales = keep.tile([P, S], U8, name="dealt_scales", align_bytes=64)
        nc.vector.tensor_copy(
            out=dealt_scales[:].rearrange("p (t m) -> p m t", t=PACK),
            in_=table_scales[:].indirect(offsets[:]),
        )
        for r in range(4):
            queue = nc.sync if r % 2 == 0 else nc.scalar
            queue.dma_start(
                out=x_scale[r:P:32, :].bitcast(I32),
                in_=dealt_scales[ROW0 + r : ROW0 + 16 : 4, :].bitcast(I32),
            )
        bias_sorted = keep.tile([P, P], F32, name="bias_sorted", align_bytes=64)
        nc.scalar.copy(
            out=bias_sorted[:].rearrange("p (t i) -> p t i", t=PACK),
            in_=bias_rows[:].rearrange("p (i t) -> p t i", t=PACK),
        )
        third = reuse.tile([P, PACK * W], F32, name="third", align_bytes=64, offset=THIRD_AT)
        fourth = reuse.tile([P, PACK * W], F32, name="fourth", align_bytes=64, offset=FOURTH_AT)
        for c, late in ((2, third), (3, fourth)):
            raw = late[:].rearrange("p (t j) -> p t j", t=PACK)
            nc.sync.dma_start(out=raw, in_=h_rows[:, :, c * W : (c + 1) * W])
            h_raw.append(raw)

        h_bf = [keep.tile([P, PACK * W], BF16, name=f"h_bf{c}", tag=tag, align_bytes=64) for c, tag in enumerate(("bf0", "bf1", "raw1"))]
        h_bf.append(reuse.tile([P, PACK * W], BF16, name="h_bf3", align_bytes=64, offset=LAST_BF_AT))
        h_codes = keep.tile([P, J], U32, name="h_codes", align_bytes=64)
        h_scale = keep.tile([P, J], U8, name="h_scale", align_bytes=64)

        def round_h(c, a, b):
            copy = nc.scalar.copy if c < ON_SCALAR else nc.vector.tensor_copy
            interleave(copy, h_bf[c][:, PACK * a : PACK * b], h_raw[c][:, :, a:b])

        def quantise_h(c, a, b):
            cols = slice(c * W + a, c * W + b)
            nc.vector.quantize_mx(out=h_codes[:, cols].bitcast(FP8X4), scales=h_scale[:, cols], in_=h_bf[c][:, PACK * a : PACK * b])

        dealt_words = keep.tile([P, S], U32, name="dealt_words", align_bytes=64)
        picked_words = keep.tile([P, S], U32, name="picked_words", align_bytes=64)
        for half in range(2):
            nc.vector.tensor_copy(
                out=picked_words[:, half * S // 2 : (half + 1) * S // 2],
                in_=table_words[:].indirect(offsets[:, half * S // 32 : (half + 1) * S // 32]),
            )
        dealt_view = dealt_words[:].bitcast(I32).rearrange("p (t a i) -> p a t i", t=PACK, i=4)
        picked_view = picked_words[:].bitcast(I32).rearrange("p (a i t) -> p a t i", t=PACK, i=4)
        for half in range(2):
            rows = slice(half * S // 32, (half + 1) * S // 32)
            nc.vector.tensor_copy(out=dealt_view[:, rows], in_=picked_view[:, rows])
        round_h(0, 0, W)
        quantise_h(0, 0, W)
        bias_turned = keep.tile([P, P], F32, name="bias_turned", tag="raw0", align_bytes=64)
        for t in (2, 3, 0, 1):
            nc.vector.transpose(bias_turned[:, 32 * t : 32 * t + 32], bias_sorted[:, 32 * t : 32 * t + 32])
        round_h(1, 0, W)
        quantise_h(1, 0, W)
        for c in range(ON_SCALAR, CHUNKS):
            for a in (0, HALF):
                round_h(c, a, a + HALF)
            for a in (0, HALF):
                quantise_h(c, a, a + HALF)

        y_codes = keep.tile([P, J], U32, name="y_codes", align_bytes=64)
        y_scale = keep.tile([P, J], U8, name="y_scale", align_bytes=64)
        y_rows = out_0.rearrange("(p t) j -> p t j", t=PACK)
        words_out = out_1[0].rearrange("p c r -> p (c r)").bitcast(I32)
        y_rounded = reuse.tile([P, PACK * J], BF16, name="y_rounded", align_bytes=64, offset=ROUNDED_AT)

        y = keep.tile([P, PACK, J], F32, name="y", align_bytes=64)

        def product(t, lo, hi, bank):
            acc = psum.tile([P, hi - lo], F32, name=f"acc{bank}", tag=f"bank{bank % BANKS}")
            nc.tensor.matmul_mx(
                out=acc[:],
                lhsT=dealt_words[:, t * P : (t + 1) * P].bitcast(FP8X4),
                lhsT_scale=x_scale[:, t * P : (t + 1) * P],
                rhs=h_codes[:, lo:hi].bitcast(FP8X4),
                rhs_scale=h_scale[:, lo:hi],
                start=True,
                stop=True,
            )
            nc.scalar.activation(out=y[:, t, lo:hi], in_=acc[:], func=GELU, bias=bias_turned[:, 32 * t + 31 : 32 * t + 32])

        def round_y(copy, lo, hi):
            interleave(copy, y_rounded[:, PACK * lo : PACK * hi], y[:, :, lo:hi])

        def quantise_y(lo, hi):
            nc.vector.quantize_mx(out=y_codes[:, lo:hi].bitcast(FP8X4), scales=y_scale[:, lo:hi], in_=y_rounded[:, PACK * lo : PACK * hi])

        def store_words(lo, hi):
            nc.sync.dma_start(out=words_out[:, lo:hi], in_=y_codes[:, lo:hi].bitcast(I32))

        bank = 0
        for step in range(CHUNKS + 1):
            first_row = 2 if step % 2 == 0 else 0
            lo, hi = max(step - 1, 0) * W, min(step + 1, CHUNKS) * W
            for a in range(lo, hi, W):
                for t in (first_row, first_row + 1):
                    product(t, a, a + W, bank)
                    bank = bank + 1
            nc.sync.dma_start(out=y_rows[:, first_row : first_row + 2, lo:hi], in_=y[:, first_row : first_row + 2, lo:hi])
            if 1 <= step < CHUNKS:
                round_y(nc.vector.tensor_copy, lo, lo + W)
            if step == CHUNKS:
                round_y(nc.vector.tensor_copy, lo, lo + HALF)
                round_y(nc.scalar.copy, lo + HALF, hi)
                quantise_y(lo - W, lo)
                quantise_y(lo, lo + HALF)
                quantise_y(lo + HALF, hi)
                store_words(2 * W, hi)
            elif 1 <= step < CHUNKS - 1:
                quantise_y(lo, lo + W)
            if step == 2:
                store_words(0, 2 * W)
        for q in range(4):
            queue = nc.scalar if q % 2 == 0 else nc.sync
            queue.dma_start(
                out=out_2[0, 4 * q : 4 * q + 4, :].bitcast(I32),
                in_=y_scale[32 * q : 32 * q + 4, :].bitcast(I32),
            )
